import numpy as np
import ml_dtypes


def mxq(x, axis, fmt="e4m3"):
    dtype, down = {"e4m3": (ml_dtypes.float8_e4m3fn, 7), "e5m2": (ml_dtypes.float8_e5m2, 14)}[fmt]
    v = np.moveaxis(np.asarray(x, np.float32).astype(ml_dtypes.bfloat16).astype(np.float64), axis, -1)
    blocks = v.reshape(v.shape[:-1] + (-1, 32))
    amax = np.abs(blocks).max(-1, keepdims=True)
    byte = np.maximum(np.where(amax > 0, np.frexp(amax)[1] - 1 + 127, 0) - down, 1)
    scale = np.exp2(byte - 127.0)
    codes = (blocks / scale).astype(np.float32).astype(dtype).astype(np.float64)
    return np.moveaxis((codes * scale).reshape(v.shape), -1, axis)


WIDE = False


def mx_kscale(k):
    if not WIDE:
        return np.ones(k)
    levels = np.array([18, -18])
    if k % 512:
        return np.exp2(np.random.permutation(np.resize(levels, k // 32))).repeat(32)
    a = np.empty((k // 512, 16))
    for p in range(k // 512):
        a[p, :8] = np.random.permutation(np.resize(levels, 8))
        for g in range(8):
            far = levels[np.abs(levels - a[p, g]) >= 10]
            a[p, g + 8] = far[np.random.randint(len(far))]
    return np.exp2(a.ravel()).repeat(32)


def f64(x):
    return np.asarray(x).astype(np.float64)


def striped(idx):
    return np.tile(np.asarray(idx).reshape(-1, 16).T, (8, 1)).astype(np.uint16)


def unstriped(offs):
    return offs[:16].T.reshape(-1).astype(np.int64)


E2M1 = np.array([0.0, 0.5, 1.0, 1.5, 2.0, 3.0, 4.0, 6.0, -0.0, -0.5, -1.0, -1.5, -2.0, -3.0, -4.0, -6.0])


def pack_weight(w, fmt):
    k, n = w.shape
    w = f64(np.asarray(w, np.float32).astype(ml_dtypes.bfloat16)).reshape(k // 32, 32, n)
    amax = np.abs(w).max(1)
    if fmt == "e4m3":
        byte = np.frexp(amax)[1] - 1 + 127 - 7
    else:
        mant, ex = np.frexp(amax / 6.0)
        byte = np.where(mant > 0.5, ex, ex - 1) + 127
    byte = np.clip(np.where(amax > 0, byte, 1), 1, 254)
    scaled = (w * np.exp2(127.0 - byte)[:, None, :]).reshape(k, n).astype(np.float32)
    by_word = np.ascontiguousarray(scaled.reshape(k // 512, 128, 4, n).transpose(0, 1, 3, 2))
    if fmt == "e4m3":
        words = by_word.astype(ml_dtypes.float8_e4m3fn).view(np.uint8)
    else:
        c = by_word.astype(ml_dtypes.float4_e2m1fn).view(np.uint8) & 0xF
        words = (c[..., 0::2] | (c[..., 1::2] << 4)).reshape(k // 512, 128, 2 * n)
    return np.ascontiguousarray(words), np.ascontiguousarray(byte.astype(np.uint8).reshape(k // 512, 16, n))


def unpack_weight(words, scales, fmt):
    g, _, n = scales.shape
    words = np.ascontiguousarray(words).reshape(g, 128, n, -1)
    if fmt == "e4m3":
        vals = words.view(ml_dtypes.float8_e4m3fn).astype(np.float64)
    else:
        nib = np.empty((g, 128, n, 4), np.uint8)
        nib[..., 0::2] = words & 0xF
        nib[..., 1::2] = words >> 4
        vals = E2M1[nib]
    vals = vals * np.repeat(np.exp2(scales.astype(np.float64) - 127.0), 8, axis=1)[..., None]
    return vals.transpose(0, 1, 3, 2).reshape(g * 512, n)


def planes(y):
    n, m = y.shape
    v = y.astype(np.float32).astype(ml_dtypes.bfloat16).astype(np.float64).reshape(n // 32, 32, m)
    top = np.abs(v).max(1)
    byte = np.clip(np.where(top > 0, np.frexp(top)[1] - 1 + 127 - 7, 1), 1, 254)
    codes = (v * np.exp2(127.0 - byte)[:, None, :]).reshape(n, m).astype(np.float32).astype(ml_dtypes.float8_e4m3fn).view(np.uint8)
    words = codes.reshape(n // 512, 128, 4, m).transpose(0, 1, 3, 2)
    return np.ascontiguousarray(words), np.ascontiguousarray(byte.astype(np.uint8).reshape(n // 512, 16, m))


T, C, D, DV = 1024, 2048, 512, 512
BETA = 0.25


def setup_inputs():
    n = np.random.standard_normal
    grid = lambda v: np.clip(np.round(v * 16) / 16, -4, 4)
    v = mx_kscale(DV)[:, None]
    wp = pack_weight(n((DV, D)) / np.sqrt(DV) / v, "e4m3")
    return {
        "zT": (grid(n((DV, T))) * v).astype(np.float32),
        "cb": (grid(n((DV, C))) * v).astype(np.float32),
        "dyT": (grid(0.5 * n((DV, T))) * v).astype(np.float32),
        "tw": np.tile(np.random.randint(8, 33, T) / 16.0, (128, 1)).astype(np.float32),
        "w_words": wp[0],
        "w_scales": wp[1],
        "offs": striped(np.random.randint(0, C, T)),
    }


def reference(zT, cb, dyT, tw, w_words, w_scales, offs):
    e = f64(zT) - f64(cb)[:, unstriped(offs)]
    g = f64(tw)[:1] * (f64(dyT) + BETA * e)
    out_0 = unpack_weight(w_words, w_scales, "e4m3").T @ mxq(g, 0, "e5m2")
    return (out_0,) + planes(out_0)

@@ -1,0 +1,211 @@
+from contextlib import ExitStack
+
+import concourse.mybir as mybir
+from concourse.masks import make_identity
+
+T, C, D, DV = 1024, 2048, 512, 512
+BETA = 0.25
+FLOPS = 2 * DV * D * T
+BYTES = 4 * (2 * DV * T + DV * C + T) + DV * D + 16 * D + 2 * 128 * T // 16 + 4 * D * T + D * T + 16 * T
+
+F32 = mybir.dt.float32
+BF16 = mybir.dt.bfloat16
+I32 = mybir.dt.int32
+U32 = mybir.dt.uint32
+U16 = mybir.dt.uint16
+U8 = mybir.dt.uint8
+E4M3 = mybir.dt.float8_e4m3fn_x4
+E5M2 = mybir.dt.float8_e5m2_x4
+COPY = mybir.ActivationFunctionType.Copy
+MULT = mybir.AluOpType.mult
+SUBTRACT = mybir.AluOpType.subtract
+
+P = 128
+LANES = 4
+BLOCKS = DV // P
+PIECE = 128
+PIECES = T // PIECE
+CHUNK = 512
+CHUNKS = T // CHUNK
+PER_CHUNK = CHUNK // PIECE
+LOADS = (128, 128, 256, 256, 128, 128)
+EARLY_LOADS = 1
+W_AFTER = 2
+
+
+def tile_attend_gvq_pl_sw_x_kernel(
+    tc, zT, cb, dyT, tw, w_words, w_scales, offs, out_0, out_1, out_2
+):
+    nc = tc.nc
+    with ExitStack() as ctx:
+        keep = ctx.enter_context(tc.tile_pool(name="keep", bufs=1))
+        psum = ctx.enter_context(tc.psum_pool(name="psum", bufs=1))
+        banks = [psum.tile([P, CHUNK], F32, name=f"bank{k}") for k in range(PIECES)]
+        on_scalar, on_vector = nc.scalar.copy, nc.vector.tensor_copy
+
+        tw_rows = keep.tile([P, PIECE], F32, name="tw_rows")
+        nc.sync.dma_start(tw_rows[:], tw.rearrange("r (k t) -> (r k) t", t=PIECE)[0:P, :])
+        offsets = keep.tile([P, T // 16], U16, name="offsets")
+        nc.sync.dma_start(offsets[:], offs)
+
+        z_view = zT.rearrange("(b p) t -> p b t", p=P)
+        dy_view = dyT.rearrange("(b p) t -> p b t", p=P)
+        w_raw = keep.tile([P, D], U32, name="w_raw")
+        book = [keep.tile([P, C], F32, name=f"book{b}") for b in range(BLOCKS)]
+        z_piece, dy_piece = [], []
+        first = 0
+        for i, width in enumerate(LOADS):
+            if i == EARLY_LOADS:
+                for b in range(BLOCKS):
+                    nc.sync.dma_start(book[b][:], cb[b * P : (b + 1) * P, :])
+            z_sb = keep.tile([P, BLOCKS, width], F32, name=f"z{i}")
+            dy_sb = keep.tile([P, BLOCKS, width], F32, name=f"dy{i}")
+            nc.sync.dma_start(z_sb[:], z_view[:, :, first : first + width])
+            nc.sync.dma_start(dy_sb[:], dy_view[:, :, first : first + width])
+            for c0 in range(0, width, PIECE):
+                z_piece.append(z_sb[:, :, c0 : c0 + PIECE])
+                dy_piece.append(dy_sb[:, :, c0 : c0 + PIECE])
+            first = first + width
+            if i == W_AFTER:
+                nc.sync.dma_start(w_raw[:].bitcast(I32), w_words[0].rearrange("p d l -> p (d l)").bitcast(I32))
+        early_pieces = sum(LOADS[:EARLY_LOADS]) // PIECE
+
+        w_scale_raw = keep.tile([P, D], U8, name="w_scale_raw")
+        nc.vector.memset(w_scale_raw[:].bitcast(I32), 0)
+        identity = keep.tile([P, P], F32, name="identity")
+        make_identity(nc, identity[:])
+        for q in range(4):
+            nc.gpsimd.dma_start(
+                w_scale_raw[32 * q : 32 * q + 4, :].bitcast(I32), w_scales[0, 4 * q : 4 * q + 4, :].bitcast(I32)
+            )
+
+        factor = keep.tile([P, PIECES], F32, name="factor")
+        nc.tensor.transpose(banks[-1][:, 0:P], tw_rows[:], identity[:])
+        nc.scalar.activation(factor[:], banks[-1][:, 0:PIECES], COPY, scale=-BETA)
+
+        g_codes = [keep.tile([P, CHUNK], U32, name=f"g_codes{c}", align_bytes=64) for c in range(CHUNKS)]
+        g_scales = [keep.tile([P, CHUNK], U8, name=f"g_scales{c}", align_bytes=64) for c in range(CHUNKS)]
+        w_codes = keep.tile([P, LANES, P], U32, name="w_codes", align_bytes=64)
+        y_scales = keep.tile([P, T], U8, name="y_scales", align_bytes=64)
+        out_view = out_0.rearrange("(p j) t -> p j t", j=LANES)
+        words_view = out_1[0].rearrange("p t l -> p (t l)").bitcast(I32)
+
+        def add_turned(k, b, source, start, stop):
+            nc.tensor.matmul(
+                banks[k][:, b * P : (b + 1) * P], source, identity[:], start=start, stop=stop, is_transpose=True
+            )
+
+        def add_rest(k):
+            rest = keep.tile([P, BLOCKS, PIECE], F32, name=f"rest{k}", align_bytes=64)
+            nc.vector.scalar_tensor_tensor(rest[:], dy_piece[k], -1.0 / BETA, z_piece[k], MULT, SUBTRACT)
+            for b in range(BLOCKS):
+                early = k < early_pieces
+                add_turned(k, b, rest[:, b, :], early and b == 0, not early and b == BLOCKS - 1)
+
+        def round_and_turn(k):
+            rounded = keep.tile([P, 2, P, 2], BF16, name=f"rounded{k}")
+            nc.scalar.activation(
+                rounded[:], banks[k][:].rearrange("t (p u e) -> t u p e", u=2, e=2), COPY, scale=factor[:, k : k + 1]
+            )
+            pairs = rounded[:].rearrange("t u p e -> t (u p e)").bitcast(F32)
+            for u in range(2):
+                nc.tensor.transpose(banks[k][:, u * P : (u + 1) * P], pairs[:, u * P : (u + 1) * P], identity[:])
+
+        def quantise_g(k, copier):
+            c, i = divmod(k, PER_CHUNK)
+            grouped = keep.tile([P, PIECE * LANES], BF16, name=f"grouped{k}", align_bytes=64)
+            copier(
+                grouped[:].bitcast(F32).rearrange("p (t u) -> p t u", u=2),
+                banks[k][:, 0 : 2 * P].rearrange("p (u t) -> p t u", u=2),
+            )
+            cols = slice(i * PIECE, (i + 1) * PIECE)
+            nc.vector.quantize_mx(g_codes[c][:, cols].bitcast(E5M2), g_scales[c][:, cols], grouped[:])
+
+        def deal_weights():
+            nc.vector.tensor_copy(
+                w_codes[:].bitcast(I32), w_raw[:].bitcast(I32).rearrange("p (m j) -> p j m", j=LANES)
+            )
+            w_scale = keep.tile([P, LANES, P], U8, name="w_scale", tag="rest2", align_bytes=64)
+            nc.vector.tensor_copy(w_scale[:], w_scale_raw[:].rearrange("p (m j) -> p j m", j=LANES))
+            return w_scale
+
+        def multiply(c, w_scale):
+            for j in range(LANES):
+                nc.tensor.matmul_mx(
+                    banks[c * PER_CHUNK + j][:],
+                    lhsT=w_codes[:, j, :].bitcast(E4M3),
+                    lhsT_scale=w_scale[:, j, :],
+                    rhs=g_codes[c][:].bitcast(E5M2),
+                    rhs_scale=g_scales[c][:],
+                    start=True,
+                    stop=True,
+                )
+
+        def store_result(c, copiers):
+            y = keep.tile([P, LANES, CHUNK], F32, name=f"y{c}")
+            tokens = slice(c * CHUNK, (c + 1) * CHUNK)
+            for j in range(LANES):
+                copiers[j](y[:, j, :], banks[c * PER_CHUNK + j][:])
+                nc.sync.dma_start(out_view[:, j, tokens], y[:, j, :])
+            return y
+
+        def store_planes(c, y, parts):
+            y_codes = keep.tile([P, CHUNK], U32, name=f"y_codes{c}", align_bytes=64)
+            t0 = 0
+            stored = 0
+            for width, copier, store in parts:
+                y_grouped = keep.tile([P, width * LANES], BF16, name=f"y_grouped{c}_{t0}", align_bytes=64)
+                copier(
+                    y_grouped[:].rearrange("p (s i j) -> p s j i", i=4, j=LANES),
+                    y[:, :, t0 : t0 + width].rearrange("p j (s i) -> p s j i", i=4),
+                )
+                cols = slice(c * CHUNK + t0, c * CHUNK + t0 + width)
+                nc.vector.quantize_mx(y_codes[:, t0 : t0 + width].bitcast(E4M3), y_scales[:, cols], y_grouped[:])
+                t0 = t0 + width
+                if store:
+                    nc.sync.dma_start(
+                        words_view[:, c * CHUNK + stored : c * CHUNK + t0], y_codes[:, stored:t0].bitcast(I32)
+                    )
+                    stored = t0
+
+        def gather(b, t0, width, tag):
+            picked = keep.tile([P, width], F32, name=f"picked{b}_{t0}", tag=tag)
+            nc.vector.tensor_copy(picked[:], book[b][:].indirect(offsets[:, t0 // 16 : (t0 + width) // 16]))
+            for c0 in range(0, width, PIECE):
+                k = (t0 + c0) // PIECE
+                early = k < early_pieces
+                add_turned(k, b, picked[:, c0 : c0 + PIECE], not early and b == 0, early and b == BLOCKS - 1)
+
+        for k in range(early_pieces):
+            add_rest(k)
+        for b in range(BLOCKS - 1):
+            for c in range(CHUNKS):
+                gather(b, c * CHUNK, CHUNK, f"picked{b}_{c}")
+        gather(BLOCKS - 1, 0, CHUNK // 2, "last_a")
+        gather(BLOCKS - 1, CHUNK // 2, CHUNK // 2, "last_b")
+
+        word_copiers = [on_scalar] * PIECES
+        w_scale = None
+        for step in range(PIECES + 2):
+            if early_pieces <= step < PIECES:
+                add_rest(step)
+            if step == 1:
+                gather(BLOCKS - 1, CHUNK, CHUNK, "z1")
+            if 1 <= step <= PIECES:
+                round_and_turn(step - 1)
+            if step >= 2:
+                quantise_g(step - 2, word_copiers[step - 2])
+            if step == 4:
+                w_scale = deal_weights()
+            if step - 2 == PER_CHUNK - 1:
+                multiply(0, w_scale)
+        multiply(1, w_scale)
+        y_first = store_result(0, [on_scalar, on_vector, on_scalar, on_scalar])
+        store_planes(0, y_first, [(256, on_vector, False), (256, on_vector, True)])
+        y_second = store_result(1, [on_scalar, on_scalar, on_scalar, on_vector])
+        store_planes(1, y_second, [(128, on_vector, False), (128, on_vector, True), (128, on_scalar, False), (128, on_scalar, True)])
+        for q in range(4):
+            engine = nc.sync if q % 2 == 0 else nc.scalar
+            engine.dma_start(
+                out_2[0, 4 * q : 4 * q + 4, :].bitcast(I32), y_scales[32 * q : 32 * q + 4, :].bitcast(I32)
+            )

@@ -19,18 +19,21 @@ E5M2 = mybir.dt.float8_e5m2_x4
 COPY = mybir.ActivationFunctionType.Copy
 MULT = mybir.AluOpType.mult
 SUBTRACT = mybir.AluOpType.subtract
+ADD = mybir.AluOpType.add
 
 P = 128
 LANES = 4
-BLOCKS = DV // P
 PIECE = 128
 PIECES = T // PIECE
 CHUNK = 512
 CHUNKS = T // CHUNK
 PER_CHUNK = CHUNK // PIECE
-LOADS = (128, 128, 256, 256, 128, 128)
+KIND = "ttsdttsd"
+LOADS = (128, 256, 256, 128, 128, 128)
 EARLY_LOADS = 1
+BOOK_FIRST = 0
 W_AFTER = 2
+PAIR_BANK = {}
 
 
 def tile_attend_gvq_pl_sw_x_kernel(
@@ -48,18 +51,21 @@ def tile_attend_gvq_pl_sw_x_kernel(
         offsets = keep.tile([P, T // 16], U16, name="offsets")
         nc.sync.dma_start(offsets[:], offs)
 
-        z_view = zT.rearrange("(b p) t -> p b t", p=P)
-        dy_view = dyT.rearrange("(b p) t -> p b t", p=P)
+        z_view = zT.rearrange("(p j) t -> p j t", j=LANES)
+        dy_view = dyT.rearrange("(p j) t -> p j t", j=LANES)
+        cb_view = cb.rearrange("(p j) c -> p j c", j=LANES)
         w_raw = keep.tile([P, D], U32, name="w_raw")
-        book = [keep.tile([P, C], F32, name=f"book{b}") for b in range(BLOCKS)]
+        book = [keep.tile([P, C], F32, name=f"book{j}") for j in range(LANES)]
         z_piece, dy_piece = [], []
         first = 0
+        for j in range(BOOK_FIRST):
+            nc.sync.dma_start(book[j][:], cb_view[:, j, :])
         for i, width in enumerate(LOADS):
             if i == EARLY_LOADS:
-                for b in range(BLOCKS):
-                    nc.sync.dma_start(book[b][:], cb[b * P : (b + 1) * P, :])
-            z_sb = keep.tile([P, BLOCKS, width], F32, name=f"z{i}")
-            dy_sb = keep.tile([P, BLOCKS, width], F32, name=f"dy{i}")
+                for j in range(BOOK_FIRST, LANES):
+                    nc.sync.dma_start(book[j][:], cb_view[:, j, :])
+            z_sb = keep.tile([P, LANES, width], F32, name=f"z{i}")
+            dy_sb = keep.tile([P, LANES, width], F32, name=f"dy{i}")
             nc.sync.dma_start(z_sb[:], z_view[:, :, first : first + width])
             nc.sync.dma_start(dy_sb[:], dy_view[:, :, first : first + width])
             for c0 in range(0, width, PIECE):
@@ -82,6 +88,15 @@ def tile_attend_gvq_pl_sw_x_kernel(
         factor = keep.tile([P, PIECES], F32, name="factor")
         nc.tensor.transpose(banks[-1][:, 0:P], tw_rows[:], identity[:])
         nc.scalar.activation(factor[:], banks[-1][:, 0:PIECES], COPY, scale=-BETA)
+        spread = {}
+        for k in range(PIECES):
+            if KIND[k] == "d":
+                spread[k] = keep.tile([P, LANES, PIECE], F32, name=f"spread{k}")
+                for j in range(LANES):
+                    nc.tensor.transpose(
+                        banks[k][:, j * P : (j + 1) * P], factor[:, k : k + 1].to_broadcast([P, P]), identity[:]
+                    )
+                nc.scalar.copy(spread[k][:].rearrange("p j t -> p (j t)"), banks[k][:])
 
         g_codes = [keep.tile([P, CHUNK], U32, name=f"g_codes{c}", align_bytes=64) for c in range(CHUNKS)]
         g_scales = [keep.tile([P, CHUNK], U8, name=f"g_scales{c}", align_bytes=64) for c in range(CHUNKS)]
@@ -90,47 +105,92 @@ def tile_attend_gvq_pl_sw_x_kernel(
         out_view = out_0.rearrange("(p j) t -> p j t", j=LANES)
         words_view = out_1[0].rearrange("p t l -> p (t l)").bitcast(I32)
 
-        def add_turned(k, b, source, start, stop):
-            nc.tensor.matmul(
-                banks[k][:, b * P : (b + 1) * P], source, identity[:], start=start, stop=stop, is_transpose=True
-            )
+        def add_turned(k, j, source, first, last):
+            if KIND[k] == "s":
+                target = banks[k + j // 2][:, j % 2 * P : (j % 2 + 1) * P]
+                start, stop = first and j % 2 == 0, last and j % 2 == 1
+            else:
+                target = banks[k][:, j * P : (j + 1) * P]
+                start, stop = first and j == 0, last and j == LANES - 1
+            nc.tensor.matmul(target, source, identity[:], start=start, stop=stop, is_transpose=True)
 
         def add_rest(k):
-            rest = keep.tile([P, BLOCKS, PIECE], F32, name=f"rest{k}", align_bytes=64)
-            nc.vector.scalar_tensor_tensor(rest[:], dy_piece[k], -1.0 / BETA, z_piece[k], MULT, SUBTRACT)
-            for b in range(BLOCKS):
-                early = k < early_pieces
-                add_turned(k, b, rest[:, b, :], early and b == 0, not early and b == BLOCKS - 1)
+            rest = keep.tile([P, LANES, PIECE], F32, name=f"rest{k}", align_bytes=64)
+            group = 2 if KIND[k] == "s" else LANES
+            for j0 in range(0, LANES, group):
+                planes = slice(j0, j0 + group)
+                nc.vector.scalar_tensor_tensor(
+                    rest[:, planes, :], dy_piece[k][:, planes, :], -1.0 / BETA, z_piece[k][:, planes, :], MULT, SUBTRACT
+                )
+                for j in range(j0, j0 + group):
+                    add_turned(k, j, rest[:, j, :], k < early_pieces, k >= early_pieces)
 
         def round_and_turn(k):
             rounded = keep.tile([P, 2, P, 2], BF16, name=f"rounded{k}")
-            nc.scalar.activation(
-                rounded[:], banks[k][:].rearrange("t (p u e) -> t u p e", u=2, e=2), COPY, scale=factor[:, k : k + 1]
-            )
             pairs = rounded[:].rearrange("t u p e -> t (u p e)").bitcast(F32)
+            scale = factor[:, k : k + 1]
+            if KIND[k] == "t":
+                nc.scalar.activation(
+                    rounded[:], banks[k][:].rearrange("t (u e p) -> t u p e", u=2, e=2), COPY, scale=scale
+                )
             for u in range(2):
-                nc.tensor.transpose(banks[k][:, u * P : (u + 1) * P], pairs[:, u * P : (u + 1) * P], identity[:])
+                if KIND[k] == "s":
+                    nc.scalar.activation(
+                        rounded[:, u, :, :],
+                        banks[k + u][:, 0 : 2 * P].rearrange("t (e p) -> t p e", e=2),
+                        COPY,
+                        scale=scale,
+                    )
+                nc.tensor.transpose(
+                    banks[PAIR_BANK.get(k, k)][:, u * P : (u + 1) * P], pairs[:, u * P : (u + 1) * P], identity[:]
+                )
 
-        def quantise_g(k, copier):
+        def quantise_g(k, grouped):
             c, i = divmod(k, PER_CHUNK)
+            cols = slice(i * PIECE, (i + 1) * PIECE)
+            nc.vector.quantize_mx(g_codes[c][:, cols].bitcast(E5M2), g_scales[c][:, cols], grouped[:])
+
+        def regroup(k, copier):
             grouped = keep.tile([P, PIECE * LANES], BF16, name=f"grouped{k}", align_bytes=64)
             copier(
                 grouped[:].bitcast(F32).rearrange("p (t u) -> p t u", u=2),
-                banks[k][:, 0 : 2 * P].rearrange("p (u t) -> p t u", u=2),
+                banks[PAIR_BANK.get(k, k)][:, 0 : 2 * P].rearrange("p (u t) -> p t u", u=2),
             )
-            cols = slice(i * PIECE, (i + 1) * PIECE)
-            nc.vector.quantize_mx(g_codes[c][:, cols].bitcast(E5M2), g_scales[c][:, cols], grouped[:])
+            quantise_g(k, grouped)
+
+        def direct_gap(k):
+            c, i = divmod(k, PER_CHUNK)
+            gap = keep.tile([P, LANES, PIECE], F32, name=f"gap{k}", align_bytes=64)
+            nc.vector.tensor_tensor(gap[:], picked[c][:, :, i * PIECE : (i + 1) * PIECE], z_piece[k], SUBTRACT)
+            return gap
+
+        def direct_g(k, gap):
+            total = keep.tile([P, LANES, PIECE], F32, name=f"total{k}", align_bytes=64)
+            grouped = keep.tile([P, PIECE * LANES], BF16, name=f"grouped{k}", align_bytes=64)
+            halves = [slice(0, PIECE // 2), slice(PIECE // 2, PIECE)]
+            for half in halves:
+                nc.vector.scalar_tensor_tensor(
+                    total[:, :, half], dy_piece[k][:, :, half], -1.0 / BETA, gap[:, :, half], MULT, ADD
+                )
+            for half in halves:
+                nc.vector.tensor_tensor(
+                    grouped[:, LANES * half.start : LANES * half.stop].rearrange("p (s i j) -> p s j i", i=4, j=LANES),
+                    total[:, :, half].rearrange("p j (s i) -> p s j i", i=4),
+                    spread[k][:, :, half].rearrange("p j (s i) -> p s j i", i=4),
+                    MULT,
+                )
+            quantise_g(k, grouped)
 
         def deal_weights():
             nc.vector.tensor_copy(
                 w_codes[:].bitcast(I32), w_raw[:].bitcast(I32).rearrange("p (m j) -> p j m", j=LANES)
             )
-            w_scale = keep.tile([P, LANES, P], U8, name="w_scale", tag="rest2", align_bytes=64)
+            w_scale = keep.tile([P, LANES, P], U8, name="w_scale", tag="rest1", align_bytes=64)
             nc.vector.tensor_copy(w_scale[:], w_scale_raw[:].rearrange("p (m j) -> p j m", j=LANES))
             return w_scale
 
-        def multiply(c, w_scale):
-            for j in range(LANES):
+        def multiply(c, w_scale, lanes):
+            for j in lanes:
                 nc.tensor.matmul_mx(
                     banks[c * PER_CHUNK + j][:],
                     lhsT=w_codes[:, j, :].bitcast(E4M3),
@@ -141,13 +201,11 @@ def tile_attend_gvq_pl_sw_x_kernel(
                     stop=True,
                 )
 
-        def store_result(c, copiers):
-            y = keep.tile([P, LANES, CHUNK], F32, name=f"y{c}")
+        def store_result(c, y, lanes, copiers):
             tokens = slice(c * CHUNK, (c + 1) * CHUNK)
-            for j in range(LANES):
+            for j in lanes:
                 copiers[j](y[:, j, :], banks[c * PER_CHUNK + j][:])
                 nc.sync.dma_start(out_view[:, j, tokens], y[:, j, :])
-            return y
 
         def store_planes(c, y, parts):
             y_codes = keep.tile([P, CHUNK], U32, name=f"y_codes{c}", align_bytes=64)
@@ -168,42 +226,54 @@ def tile_attend_gvq_pl_sw_x_kernel(
                     )
                     stored = t0
 
-        def gather(b, t0, width, tag):
-            picked = keep.tile([P, width], F32, name=f"picked{b}_{t0}", tag=tag)
-            nc.vector.tensor_copy(picked[:], book[b][:].indirect(offsets[:, t0 // 16 : (t0 + width) // 16]))
+        def gather(j, t0, width):
+            c, c0 = divmod(t0, CHUNK)
+            target = picked[c][:, j, c0 : c0 + width]
+            nc.vector.tensor_copy(target, book[j][:].indirect(offsets[:, t0 // 16 : (t0 + width) // 16]))
             for c0 in range(0, width, PIECE):
                 k = (t0 + c0) // PIECE
-                early = k < early_pieces
-                add_turned(k, b, picked[:, c0 : c0 + PIECE], not early and b == 0, early and b == BLOCKS - 1)
+                if KIND[k] != "d":
+                    add_turned(k, j, target[:, c0 : c0 + PIECE], k >= early_pieces, k < early_pieces)
 
+        picked = [keep.tile([P, LANES, CHUNK], F32, name=f"picked{c}") for c in range(CHUNKS)]
         for k in range(early_pieces):
             add_rest(k)
-        for b in range(BLOCKS - 1):
+        for j in range(LANES - 1):
             for c in range(CHUNKS):
-                gather(b, c * CHUNK, CHUNK, f"picked{b}_{c}")
-        gather(BLOCKS - 1, 0, CHUNK // 2, "last_a")
-        gather(BLOCKS - 1, CHUNK // 2, CHUNK // 2, "last_b")
+                gather(j, c * CHUNK, CHUNK)
+        gather(LANES - 1, 0, CHUNK // 2)
+        gather(LANES - 1, CHUNK // 2, CHUNK // 2)
 
-        word_copiers = [on_scalar] * PIECES
+        word_copiers = [on_scalar] * 6 + [on_vector] * 2
         w_scale = None
+        gaps = {}
+        y = [keep.tile([P, LANES, CHUNK], F32, name=f"y{c}") for c in range(CHUNKS)]
         for step in range(PIECES + 2):
             if early_pieces <= step < PIECES:
-                add_rest(step)
+                if KIND[step] == "d":
+                    gaps[step] = direct_gap(step)
+                else:
+                    add_rest(step)
             if step == 1:
-                gather(BLOCKS - 1, CHUNK, CHUNK, "z1")
-            if 1 <= step <= PIECES:
+                gather(LANES - 1, CHUNK, CHUNK)
+            if 1 <= step <= PIECES and KIND[step - 1] != "d":
                 round_and_turn(step - 1)
-            if step >= 2:
-                quantise_g(step - 2, word_copiers[step - 2])
-            if step == 4:
+            if step - 0 in gaps:
+                direct_g(step - 0, gaps[step - 0])
+            if step >= 2 and KIND[step - 2] != "d":
+                regroup(step - 2, word_copiers[step - 2])
+            if step == 3:
                 w_scale = deal_weights()
-            if step - 2 == PER_CHUNK - 1:
-                multiply(0, w_scale)
-        multiply(1, w_scale)
-        y_first = store_result(0, [on_scalar, on_vector, on_scalar, on_scalar])
-        store_planes(0, y_first, [(256, on_vector, False), (256, on_vector, True)])
-        y_second = store_result(1, [on_scalar, on_scalar, on_scalar, on_vector])
-        store_planes(1, y_second, [(128, on_vector, False), (128, on_vector, True), (128, on_scalar, False), (128, on_scalar, True)])
+            if step == 5:
+                multiply(0, w_scale, range(2))
+            if step == 6:
+                store_result(0, y[0], range(1), [on_scalar, on_scalar, on_scalar, on_vector])
+        multiply(0, w_scale, range(2, LANES))
+        multiply(1, w_scale, range(LANES))
+        store_result(0, y[0], range(1, LANES), [on_scalar, on_scalar, on_scalar, on_vector])
+        store_planes(0, y[0], [(256, on_vector, False), (256, on_scalar, True)])
+        store_result(1, y[1], range(LANES), [on_scalar, on_vector, on_scalar, on_vector])
+        store_planes(1, y[1], [(256, on_vector, False), (128, on_scalar, False), (128, on_vector, True)])
         for q in range(4):
             engine = nc.sync if q % 2 == 0 else nc.scalar
             engine.dma_start(

@@ -18,7 +18,6 @@ E4M3 = mybir.dt.float8_e4m3fn_x4
 E5M2 = mybir.dt.float8_e5m2_x4
 COPY = mybir.ActivationFunctionType.Copy
 MULT = mybir.AluOpType.mult
-SUBTRACT = mybir.AluOpType.subtract
 ADD = mybir.AluOpType.add
 
 P = 128
@@ -28,12 +27,9 @@ PIECES = T // PIECE
 CHUNK = 512
 CHUNKS = T // CHUNK
 PER_CHUNK = CHUNK // PIECE
-KIND = "ttsdttsd"
-LOADS = (128, 256, 256, 128, 128, 128)
-EARLY_LOADS = 1
-BOOK_FIRST = 0
-W_AFTER = 2
-PAIR_BANK = {}
+KIND = "ppppttsd"
+LOADS = (("cb", 0, 2), ("z", 0, 1), ("dy", 0, 1), ("cb", 2, 2), ("z", 1, 1), ("dy", 1, 1), ("z", 2, 2), ("dy", 2, 2), ("w", 0, 1), ("z", 4, 1), ("dy", 4, 1), ("z", 5, 1), ("dy", 5, 1), ("z", 6, 1), ("dy", 6, 1), ("z", 7, 1), ("dy", 7, 1))
+PAIR_BANK = {5: 3}
 
 
 def tile_attend_gvq_pl_sw_x_kernel(
@@ -56,38 +52,42 @@ def tile_attend_gvq_pl_sw_x_kernel(
         cb_view = cb.rearrange("(p j) c -> p j c", j=LANES)
         w_raw = keep.tile([P, D], U32, name="w_raw")
         book = [keep.tile([P, C], F32, name=f"book{j}") for j in range(LANES)]
-        z_piece, dy_piece = [], []
-        first = 0
-        for j in range(BOOK_FIRST):
-            nc.sync.dma_start(book[j][:], cb_view[:, j, :])
-        for i, width in enumerate(LOADS):
-            if i == EARLY_LOADS:
-                for j in range(BOOK_FIRST, LANES):
-                    nc.sync.dma_start(book[j][:], cb_view[:, j, :])
-            z_sb = keep.tile([P, LANES, width], F32, name=f"z{i}")
-            dy_sb = keep.tile([P, LANES, width], F32, name=f"dy{i}")
-            nc.sync.dma_start(z_sb[:], z_view[:, :, first : first + width])
-            nc.sync.dma_start(dy_sb[:], dy_view[:, :, first : first + width])
-            for c0 in range(0, width, PIECE):
-                z_piece.append(z_sb[:, :, c0 : c0 + PIECE])
-                dy_piece.append(dy_sb[:, :, c0 : c0 + PIECE])
-            first = first + width
-            if i == W_AFTER:
-                nc.sync.dma_start(w_raw[:].bitcast(I32), w_words[0].rearrange("p d l -> p (d l)").bitcast(I32))
-        early_pieces = sum(LOADS[:EARLY_LOADS]) // PIECE
-
         w_scale_raw = keep.tile([P, D], U8, name="w_scale_raw")
         nc.vector.memset(w_scale_raw[:].bitcast(I32), 0)
+        z_piece, dy_piece = {}, {}
+        early_pieces = None
+        for what, k0, count in LOADS:
+            if what == "cb":
+                for j in range(k0, k0 + count):
+                    nc.sync.dma_start(book[j][:], cb_view[:, j, :])
+                early_pieces = len(dy_piece)
+            elif what == "s":
+                for q in range(4):
+                    nc.sync.dma_start(
+                        w_scale_raw[32 * q : 32 * q + 4, :].bitcast(I32),
+                        w_scales[0, 4 * q : 4 * q + 4, :].bitcast(I32),
+                    )
+            elif what == "w":
+                nc.sync.dma_start(w_raw[:].bitcast(I32), w_words[0].rearrange("p d l -> p (d l)").bitcast(I32))
+            else:
+                view, pieces = (z_view, z_piece) if what == "z" else (dy_view, dy_piece)
+                loaded = keep.tile([P, LANES, count * PIECE], F32, name=f"{what}{k0}", align_bytes=64)
+                nc.sync.dma_start(loaded[:], view[:, :, k0 * PIECE : (k0 + count) * PIECE])
+                for i in range(count):
+                    pieces[k0 + i] = loaded[:, :, i * PIECE : (i + 1) * PIECE]
+
         identity = keep.tile([P, P], F32, name="identity")
         make_identity(nc, identity[:])
-        for q in range(4):
-            nc.gpsimd.dma_start(
-                w_scale_raw[32 * q : 32 * q + 4, :].bitcast(I32), w_scales[0, 4 * q : 4 * q + 4, :].bitcast(I32)
-            )
 
+        if all(what != "s" for what, k0, count in LOADS):
+            for q in range(4):
+                nc.gpsimd.dma_start(
+                    w_scale_raw[32 * q : 32 * q + 4, :].bitcast(I32), w_scales[0, 4 * q : 4 * q + 4, :].bitcast(I32)
+                )
+        ahead = max(early_pieces, 3)
         factor = keep.tile([P, PIECES], F32, name="factor")
         nc.tensor.transpose(banks[-1][:, 0:P], tw_rows[:], identity[:])
-        nc.scalar.activation(factor[:], banks[-1][:, 0:PIECES], COPY, scale=-BETA)
+        nc.scalar.activation(factor[:], banks[-1][:, 0:PIECES], COPY)
         spread = {}
         for k in range(PIECES):
             if KIND[k] == "d":
@@ -116,20 +116,28 @@ def tile_attend_gvq_pl_sw_x_kernel(
 
         def add_rest(k):
             rest = keep.tile([P, LANES, PIECE], F32, name=f"rest{k}", align_bytes=64)
+            early = k < early_pieces
+            if KIND[k] == "p":
+                nc.scalar.activation(rest[:], z_piece[k], COPY, scale=BETA)
+                for j in range(LANES):
+                    add_turned(k, j, rest[:, j, :], early, False)
+                for j in range(LANES):
+                    add_turned(k, j, dy_piece[k][:, j, :], False, k >= ahead)
+                return
             group = 2 if KIND[k] == "s" else LANES
             for j0 in range(0, LANES, group):
                 planes = slice(j0, j0 + group)
                 nc.vector.scalar_tensor_tensor(
-                    rest[:, planes, :], dy_piece[k][:, planes, :], -1.0 / BETA, z_piece[k][:, planes, :], MULT, SUBTRACT
+                    rest[:, planes, :], z_piece[k][:, planes, :], BETA, dy_piece[k][:, planes, :], MULT, ADD
                 )
                 for j in range(j0, j0 + group):
-                    add_turned(k, j, rest[:, j, :], k < early_pieces, k >= early_pieces)
+                    add_turned(k, j, rest[:, j, :], early, k >= ahead)
 
         def round_and_turn(k):
-            rounded = keep.tile([P, 2, P, 2], BF16, name=f"rounded{k}")
+            rounded = keep.tile([P, 2, P, 2], BF16, name=f"rounded{k}", align_bytes=64)
             pairs = rounded[:].rearrange("t u p e -> t (u p e)").bitcast(F32)
             scale = factor[:, k : k + 1]
-            if KIND[k] == "t":
+            if KIND[k] != "s":
                 nc.scalar.activation(
                     rounded[:], banks[k][:].rearrange("t (u e p) -> t u p e", u=2, e=2), COPY, scale=scale
                 )
@@ -151,7 +159,7 @@ def tile_attend_gvq_pl_sw_x_kernel(
             nc.vector.quantize_mx(g_codes[c][:, cols].bitcast(E5M2), g_scales[c][:, cols], grouped[:])
 
         def regroup(k, copier):
-            grouped = keep.tile([P, PIECE * LANES], BF16, name=f"grouped{k}", align_bytes=64)
+            grouped = keep.tile([P, PIECE * LANES], BF16, name=f"grouped{k}", tag=(f"rest{k + 0}" if 0 and k + 0 < PIECES and KIND[k + 0] != "d" else f"grouped{k}"), align_bytes=64)
             copier(
                 grouped[:].bitcast(F32).rearrange("p (t u) -> p t u", u=2),
                 banks[PAIR_BANK.get(k, k)][:, 0 : 2 * P].rearrange("p (u t) -> p t u", u=2),
@@ -161,7 +169,11 @@ def tile_attend_gvq_pl_sw_x_kernel(
         def direct_gap(k):
             c, i = divmod(k, PER_CHUNK)
             gap = keep.tile([P, LANES, PIECE], F32, name=f"gap{k}", align_bytes=64)
-            nc.vector.tensor_tensor(gap[:], picked[c][:, :, i * PIECE : (i + 1) * PIECE], z_piece[k], SUBTRACT)
+            cols = slice(i * PIECE, (i + 1) * PIECE)
+            nc.vector.scalar_tensor_tensor(
+                gap[:, 0:3, :], z_piece[k][:, 0:3, :], BETA, picked[c][:, :, cols], MULT, ADD
+            )
+            nc.vector.scalar_tensor_tensor(gap[:, 3, :], z_piece[k][:, 3, :], BETA, last[c][:, cols], MULT, ADD)
             return gap
 
         def direct_g(k, gap):
@@ -169,14 +181,12 @@ def tile_attend_gvq_pl_sw_x_kernel(
             grouped = keep.tile([P, PIECE * LANES], BF16, name=f"grouped{k}", align_bytes=64)
             halves = [slice(0, PIECE // 2), slice(PIECE // 2, PIECE)]
             for half in halves:
-                nc.vector.scalar_tensor_tensor(
-                    total[:, :, half], dy_piece[k][:, :, half], -1.0 / BETA, gap[:, :, half], MULT, ADD
-                )
+                nc.vector.tensor_tensor(total[:, :, half], dy_piece[k][:, :, half], gap[:, :, half], ADD)
             for half in halves:
                 nc.vector.tensor_tensor(
-                    grouped[:, LANES * half.start : LANES * half.stop].rearrange("p (s i j) -> p s j i", i=4, j=LANES),
-                    total[:, :, half].rearrange("p j (s i) -> p s j i", i=4),
-                    spread[k][:, :, half].rearrange("p j (s i) -> p s j i", i=4),
+                    grouped[:, LANES * half.start : LANES * half.stop].rearrange("p (s i j) -> p s j i", i=2, j=LANES),
+                    total[:, :, half].rearrange("p j (s i) -> p s j i", i=2),
+                    spread[k][:, :, half].rearrange("p j (s i) -> p s j i", i=2),
                     MULT,
                 )
             quantise_g(k, grouped)
@@ -185,7 +195,7 @@ def tile_attend_gvq_pl_sw_x_kernel(
             nc.vector.tensor_copy(
                 w_codes[:].bitcast(I32), w_raw[:].bitcast(I32).rearrange("p (m j) -> p j m", j=LANES)
             )
-            w_scale = keep.tile([P, LANES, P], U8, name="w_scale", tag="rest1", align_bytes=64)
+            w_scale = keep.tile([P, LANES, P], U8, name="w_scale", tag="rest2", align_bytes=64)
             nc.vector.tensor_copy(w_scale[:], w_scale_raw[:].rearrange("p (m j) -> p j m", j=LANES))
             return w_scale
 
@@ -214,8 +224,8 @@ def tile_attend_gvq_pl_sw_x_kernel(
             for width, copier, store in parts:
                 y_grouped = keep.tile([P, width * LANES], BF16, name=f"y_grouped{c}_{t0}", align_bytes=64)
                 copier(
-                    y_grouped[:].rearrange("p (s i j) -> p s j i", i=4, j=LANES),
-                    y[:, :, t0 : t0 + width].rearrange("p j (s i) -> p s j i", i=4),
+                    y_grouped[:].rearrange("p (s i j) -> p s j i", i=2, j=LANES),
+                    y[:, :, t0 : t0 + width].rearrange("p j (s i) -> p s j i", i=2),
                 )
                 cols = slice(c * CHUNK + t0, c * CHUNK + t0 + width)
                 nc.vector.quantize_mx(y_codes[:, t0 : t0 + width].bitcast(E4M3), y_scales[:, cols], y_grouped[:])
@@ -226,54 +236,58 @@ def tile_attend_gvq_pl_sw_x_kernel(
                     )
                     stored = t0
 
-        def gather(j, t0, width):
-            c, c0 = divmod(t0, CHUNK)
-            target = picked[c][:, j, c0 : c0 + width]
-            nc.vector.tensor_copy(target, book[j][:].indirect(offsets[:, t0 // 16 : (t0 + width) // 16]))
-            for c0 in range(0, width, PIECE):
-                k = (t0 + c0) // PIECE
+        def gather(j, c, target):
+            codes = offsets[:, c * CHUNK // 16 : (c + 1) * CHUNK // 16]
+            nc.vector.tensor_scalar(target, book[j][:].indirect(codes), -BETA, 0.0, MULT, ADD)
+            for i in range(PER_CHUNK):
+                k = c * PER_CHUNK + i
                 if KIND[k] != "d":
-                    add_turned(k, j, target[:, c0 : c0 + PIECE], k >= early_pieces, k < early_pieces)
+                    add_turned(k, j, target[:, i * PIECE : (i + 1) * PIECE], k >= early_pieces, k < ahead)
 
-        picked = [keep.tile([P, LANES, CHUNK], F32, name=f"picked{c}") for c in range(CHUNKS)]
+        picked = [keep.tile([P, LANES - 1, CHUNK], F32, name=f"picked{c}") for c in range(CHUNKS)]
+        last = [keep.tile([P, CHUNK], F32, name="picked_last0")]
         for k in range(early_pieces):
             add_rest(k)
         for j in range(LANES - 1):
             for c in range(CHUNKS):
-                gather(j, c * CHUNK, CHUNK)
-        gather(LANES - 1, 0, CHUNK // 2)
-        gather(LANES - 1, CHUNK // 2, CHUNK // 2)
+                gather(j, c, picked[c][:, j, :])
+        for k in range(early_pieces, ahead):
+            add_rest(k)
+        gather(LANES - 1, 0, last[0][:])
 
-        word_copiers = [on_scalar] * 6 + [on_vector] * 2
+        word_copiers = [on_scalar] * PIECES
         w_scale = None
         gaps = {}
-        y = [keep.tile([P, LANES, CHUNK], F32, name=f"y{c}") for c in range(CHUNKS)]
+        y = {}
         for step in range(PIECES + 2):
-            if early_pieces <= step < PIECES:
+            if ahead <= step < PIECES:
                 if KIND[step] == "d":
                     gaps[step] = direct_gap(step)
                 else:
                     add_rest(step)
-            if step == 1:
-                gather(LANES - 1, CHUNK, CHUNK)
+            if step == 3:
+                last.append(keep.tile([P, CHUNK], F32, name="picked_last1", tag="z1", align_bytes=64))
+                gather(LANES - 1, 1, last[1][:])
             if 1 <= step <= PIECES and KIND[step - 1] != "d":
                 round_and_turn(step - 1)
             if step - 0 in gaps:
                 direct_g(step - 0, gaps[step - 0])
             if step >= 2 and KIND[step - 2] != "d":
                 regroup(step - 2, word_copiers[step - 2])
-            if step == 3:
+            if step == 2:
                 w_scale = deal_weights()
             if step == 5:
                 multiply(0, w_scale, range(2))
-            if step == 6:
-                store_result(0, y[0], range(1), [on_scalar, on_scalar, on_scalar, on_vector])
+            if step == 7:
+                y[0] = keep.tile([P, LANES, CHUNK], F32, name="y0", tag="rest4", align_bytes=64)
+                store_result(0, y[0], range(2), [on_scalar] * 4)
         multiply(0, w_scale, range(2, LANES))
         multiply(1, w_scale, range(LANES))
-        store_result(0, y[0], range(1, LANES), [on_scalar, on_scalar, on_scalar, on_vector])
-        store_planes(0, y[0], [(256, on_vector, False), (256, on_scalar, True)])
-        store_result(1, y[1], range(LANES), [on_scalar, on_vector, on_scalar, on_vector])
-        store_planes(1, y[1], [(256, on_vector, False), (128, on_scalar, False), (128, on_vector, True)])
+        store_result(0, y[0], range(2, LANES), [on_scalar] * 4)
+        store_planes(0, y[0], [(256, on_vector, False), (256, on_vector, True)])
+        y[1] = keep.tile([P, LANES, CHUNK], F32, name="y1")
+        store_result(1, y[1], range(LANES), [on_scalar] * 4)
+        store_planes(1, y[1], [(128, on_vector, False), (128, on_vector, True), (128, on_scalar, False), (128, on_scalar, True)])
         for q in range(4):
             engine = nc.sync if q % 2 == 0 else nc.scalar
             engine.dma_start(

@@ -22,14 +22,19 @@ ADD = mybir.AluOpType.add
 
 P = 128
 LANES = 4
+QUADRANTS = 4
 PIECE = 128
 PIECES = T // PIECE
 CHUNK = 512
-CHUNKS = T // CHUNK
 PER_CHUNK = CHUNK // PIECE
-KIND = "ppppttsd"
-LOADS = (("cb", 0, 2), ("z", 0, 1), ("dy", 0, 1), ("cb", 2, 2), ("z", 1, 1), ("dy", 1, 1), ("z", 2, 2), ("dy", 2, 2), ("w", 0, 1), ("z", 4, 1), ("dy", 4, 1), ("z", 5, 1), ("dy", 5, 1), ("z", 6, 1), ("dy", 6, 1), ("z", 7, 1), ("dy", 7, 1))
-PAIR_BANK = {5: 3}
+CODES_PER_COLUMN = 16
+
+DIRECT = PIECES - 1
+SPLIT = PIECES - 2
+PAIRED = 2
+PLANES_BEFORE_PRELOAD = 2
+BEFORE_LAST_PLANE = 3
+EARLY_LANES = 2
 
 
 def tile_attend_gvq_pl_sw_x_kernel(
@@ -40,11 +45,10 @@ def tile_attend_gvq_pl_sw_x_kernel(
         keep = ctx.enter_context(tc.tile_pool(name="keep", bufs=1))
         psum = ctx.enter_context(tc.psum_pool(name="psum", bufs=1))
         banks = [psum.tile([P, CHUNK], F32, name=f"bank{k}") for k in range(PIECES)]
-        on_scalar, on_vector = nc.scalar.copy, nc.vector.tensor_copy
 
         tw_rows = keep.tile([P, PIECE], F32, name="tw_rows")
         nc.sync.dma_start(tw_rows[:], tw.rearrange("r (k t) -> (r k) t", t=PIECE)[0:P, :])
-        offsets = keep.tile([P, T // 16], U16, name="offsets")
+        offsets = keep.tile([P, T // CODES_PER_COLUMN], U16, name="offsets")
         nc.sync.dma_start(offsets[:], offs)
 
         z_view = zT.rearrange("(p j) t -> p j t", j=LANES)
@@ -55,151 +59,161 @@ def tile_attend_gvq_pl_sw_x_kernel(
         w_scale_raw = keep.tile([P, D], U8, name="w_scale_raw")
         nc.vector.memset(w_scale_raw[:].bitcast(I32), 0)
         z_piece, dy_piece = {}, {}
-        early_pieces = None
-        for what, k0, count in LOADS:
-            if what == "cb":
-                for j in range(k0, k0 + count):
-                    nc.sync.dma_start(book[j][:], cb_view[:, j, :])
-                early_pieces = len(dy_piece)
-            elif what == "s":
-                for q in range(4):
-                    nc.sync.dma_start(
-                        w_scale_raw[32 * q : 32 * q + 4, :].bitcast(I32),
-                        w_scales[0, 4 * q : 4 * q + 4, :].bitcast(I32),
-                    )
-            elif what == "w":
-                nc.sync.dma_start(w_raw[:].bitcast(I32), w_words[0].rearrange("p d l -> p (d l)").bitcast(I32))
-            else:
-                view, pieces = (z_view, z_piece) if what == "z" else (dy_view, dy_piece)
-                loaded = keep.tile([P, LANES, count * PIECE], F32, name=f"{what}{k0}", align_bytes=64)
-                nc.sync.dma_start(loaded[:], view[:, :, k0 * PIECE : (k0 + count) * PIECE])
+
+        def load_book(planes):
+            for j in planes:
+                nc.sync.dma_start(book[j][:], cb_view[:, j, :])
+
+        def load_pieces(first, count):
+            for label, view, pieces in (("z", z_view, z_piece), ("dy", dy_view, dy_piece)):
+                loaded = keep.tile([P, LANES, count * PIECE], F32, name=f"{label}{first}", align_bytes=64)
+                nc.sync.dma_start(loaded[:], view[:, :, first * PIECE : (first + count) * PIECE])
                 for i in range(count):
-                    pieces[k0 + i] = loaded[:, :, i * PIECE : (i + 1) * PIECE]
+                    pieces[first + i] = loaded[:, :, i * PIECE : (i + 1) * PIECE]
+
+        load_book(range(PLANES_BEFORE_PRELOAD))
+        load_pieces(0, 1)
+        load_book(range(PLANES_BEFORE_PRELOAD, LANES))
+        load_pieces(1, 1)
+        load_pieces(PAIRED, 2)
+        nc.sync.dma_start(w_raw[:].bitcast(I32), w_words[0].rearrange("p d l -> p (d l)").bitcast(I32))
+        for k in range(PER_CHUNK, PIECES):
+            load_pieces(k, 1)
 
         identity = keep.tile([P, P], F32, name="identity")
         make_identity(nc, identity[:])
+        for q in range(QUADRANTS):
+            nc.gpsimd.dma_start(
+                w_scale_raw[32 * q : 32 * q + 4, :].bitcast(I32), w_scales[0, 4 * q : 4 * q + 4, :].bitcast(I32)
+            )
 
-        if all(what != "s" for what, k0, count in LOADS):
-            for q in range(4):
-                nc.gpsimd.dma_start(
-                    w_scale_raw[32 * q : 32 * q + 4, :].bitcast(I32), w_scales[0, 4 * q : 4 * q + 4, :].bitcast(I32)
-                )
-        ahead = max(early_pieces, 3)
-        factor = keep.tile([P, PIECES], F32, name="factor")
-        nc.tensor.transpose(banks[-1][:, 0:P], tw_rows[:], identity[:])
-        nc.scalar.activation(factor[:], banks[-1][:, 0:PIECES], COPY)
-        spread = {}
-        for k in range(PIECES):
-            if KIND[k] == "d":
-                spread[k] = keep.tile([P, LANES, PIECE], F32, name=f"spread{k}")
-                for j in range(LANES):
-                    nc.tensor.transpose(
-                        banks[k][:, j * P : (j + 1) * P], factor[:, k : k + 1].to_broadcast([P, P]), identity[:]
-                    )
-                nc.scalar.copy(spread[k][:].rearrange("p j t -> p (j t)"), banks[k][:])
+        weight = keep.tile([P, PIECES], F32, name="weight")
+        nc.tensor.transpose(banks[DIRECT][:, 0:P], tw_rows[:], identity[:])
+        nc.scalar.activation(weight[:], banks[DIRECT][:, 0:PIECES], COPY)
+        direct_weight = keep.tile([P, PIECE, LANES], F32, name="direct_weight")
+        for j in range(LANES):
+            nc.tensor.transpose(
+                banks[DIRECT][:, j * P : (j + 1) * P], weight[:, DIRECT : DIRECT + 1].to_broadcast([P, P]), identity[:]
+            )
+        nc.scalar.copy(direct_weight[:], banks[DIRECT][:].rearrange("p (j t) -> p t j", j=LANES))
 
-        g_codes = [keep.tile([P, CHUNK], U32, name=f"g_codes{c}", align_bytes=64) for c in range(CHUNKS)]
-        g_scales = [keep.tile([P, CHUNK], U8, name=f"g_scales{c}", align_bytes=64) for c in range(CHUNKS)]
+        g_codes = [keep.tile([P, CHUNK], U32, name=f"g_codes{c}", align_bytes=64) for c in range(2)]
+        g_scales = [keep.tile([P, CHUNK], U8, name=f"g_scales{c}", align_bytes=64) for c in range(2)]
         w_codes = keep.tile([P, LANES, P], U32, name="w_codes", align_bytes=64)
         y_scales = keep.tile([P, T], U8, name="y_scales", align_bytes=64)
         out_view = out_0.rearrange("(p j) t -> p j t", j=LANES)
         words_view = out_1[0].rearrange("p t l -> p (t l)").bitcast(I32)
 
-        def add_turned(k, j, source, first, last):
-            if KIND[k] == "s":
-                target = banks[k + j // 2][:, j % 2 * P : (j % 2 + 1) * P]
-                start, stop = first and j % 2 == 0, last and j % 2 == 1
-            else:
-                target = banks[k][:, j * P : (j + 1) * P]
-                start, stop = first and j == 0, last and j == LANES - 1
-            nc.tensor.matmul(target, source, identity[:], start=start, stop=stop, is_transpose=True)
+        def add_turned(k, j, source, first_term, last_term):
+            planes = 2 if k == SPLIT else LANES
+            place = j % planes
+            nc.tensor.matmul(
+                banks[k + j // planes][:, place * P : (place + 1) * P],
+                source,
+                identity[:],
+                start=first_term and place == 0,
+                stop=last_term and place == planes - 1,
+                is_transpose=True,
+            )
 
-        def add_rest(k):
+        def gather(j, c, target):
+            codes = offsets[:, c * CHUNK // CODES_PER_COLUMN : (c + 1) * CHUNK // CODES_PER_COLUMN]
+            nc.vector.tensor_scalar(target, book[j][:].indirect(codes), -BETA, 0.0, MULT, ADD)
+            for i in range(PER_CHUNK):
+                k = c * PER_CHUNK + i
+                if k != DIRECT:
+                    add_turned(k, j, target[:, i * PIECE : (i + 1) * PIECE], k > 0, k < BEFORE_LAST_PLANE)
+
+        def add_inputs(k):
             rest = keep.tile([P, LANES, PIECE], F32, name=f"rest{k}", align_bytes=64)
-            early = k < early_pieces
-            if KIND[k] == "p":
+            closes = k >= BEFORE_LAST_PLANE
+            if k < PER_CHUNK:
                 nc.scalar.activation(rest[:], z_piece[k], COPY, scale=BETA)
                 for j in range(LANES):
-                    add_turned(k, j, rest[:, j, :], early, False)
+                    add_turned(k, j, rest[:, j, :], k == 0, False)
                 for j in range(LANES):
-                    add_turned(k, j, dy_piece[k][:, j, :], False, k >= ahead)
+                    add_turned(k, j, dy_piece[k][:, j, :], False, closes)
                 return
-            group = 2 if KIND[k] == "s" else LANES
+            group = 2 if k == SPLIT else LANES
             for j0 in range(0, LANES, group):
                 planes = slice(j0, j0 + group)
                 nc.vector.scalar_tensor_tensor(
                     rest[:, planes, :], z_piece[k][:, planes, :], BETA, dy_piece[k][:, planes, :], MULT, ADD
                 )
                 for j in range(j0, j0 + group):
-                    add_turned(k, j, rest[:, j, :], early, k >= ahead)
+                    add_turned(k, j, rest[:, j, :], False, closes)
+
+        def pair_bank(k):
+            return banks[PER_CHUNK - 1] if k == SPLIT - 1 else banks[k]
 
         def round_and_turn(k):
             rounded = keep.tile([P, 2, P, 2], BF16, name=f"rounded{k}", align_bytes=64)
             pairs = rounded[:].rearrange("t u p e -> t (u p e)").bitcast(F32)
-            scale = factor[:, k : k + 1]
-            if KIND[k] != "s":
+            scale = weight[:, k : k + 1]
+            if k != SPLIT:
                 nc.scalar.activation(
                     rounded[:], banks[k][:].rearrange("t (u e p) -> t u p e", u=2, e=2), COPY, scale=scale
                 )
             for u in range(2):
-                if KIND[k] == "s":
+                if k == SPLIT:
                     nc.scalar.activation(
                         rounded[:, u, :, :],
                         banks[k + u][:, 0 : 2 * P].rearrange("t (e p) -> t p e", e=2),
                         COPY,
                         scale=scale,
                     )
-                nc.tensor.transpose(
-                    banks[PAIR_BANK.get(k, k)][:, u * P : (u + 1) * P], pairs[:, u * P : (u + 1) * P], identity[:]
-                )
+                nc.tensor.transpose(pair_bank(k)[:, u * P : (u + 1) * P], pairs[:, u * P : (u + 1) * P], identity[:])
 
         def quantise_g(k, grouped):
             c, i = divmod(k, PER_CHUNK)
             cols = slice(i * PIECE, (i + 1) * PIECE)
             nc.vector.quantize_mx(g_codes[c][:, cols].bitcast(E5M2), g_scales[c][:, cols], grouped[:])
 
-        def regroup(k, copier):
-            grouped = keep.tile([P, PIECE * LANES], BF16, name=f"grouped{k}", tag=(f"rest{k + 0}" if 0 and k + 0 < PIECES and KIND[k + 0] != "d" else f"grouped{k}"), align_bytes=64)
-            copier(
+        def regroup(k):
+            grouped = keep.tile([P, PIECE * LANES], BF16, name=f"grouped{k}", align_bytes=64)
+            nc.scalar.copy(
                 grouped[:].bitcast(F32).rearrange("p (t u) -> p t u", u=2),
-                banks[PAIR_BANK.get(k, k)][:, 0 : 2 * P].rearrange("p (u t) -> p t u", u=2),
+                pair_bank(k)[:, 0 : 2 * P].rearrange("p (u t) -> p t u", u=2),
             )
             quantise_g(k, grouped)
 
-        def direct_gap(k):
-            c, i = divmod(k, PER_CHUNK)
-            gap = keep.tile([P, LANES, PIECE], F32, name=f"gap{k}", align_bytes=64)
-            cols = slice(i * PIECE, (i + 1) * PIECE)
+        def direct_gap():
+            cols = slice(CHUNK - PIECE, CHUNK)
+            z = z_piece[DIRECT]
+            gap = keep.tile([P, LANES, PIECE], F32, name="gap", align_bytes=64)
             nc.vector.scalar_tensor_tensor(
-                gap[:, 0:3, :], z_piece[k][:, 0:3, :], BETA, picked[c][:, :, cols], MULT, ADD
+                gap[:, 0 : LANES - 1, :], z[:, 0 : LANES - 1, :], BETA, picked[1][:, :, cols], MULT, ADD
             )
-            nc.vector.scalar_tensor_tensor(gap[:, 3, :], z_piece[k][:, 3, :], BETA, last[c][:, cols], MULT, ADD)
+            nc.vector.scalar_tensor_tensor(
+                gap[:, LANES - 1, :], z[:, LANES - 1, :], BETA, picked_last[1][:, cols], MULT, ADD
+            )
             return gap
 
-        def direct_g(k, gap):
-            total = keep.tile([P, LANES, PIECE], F32, name=f"total{k}", align_bytes=64)
-            grouped = keep.tile([P, PIECE * LANES], BF16, name=f"grouped{k}", align_bytes=64)
+        def direct_g(gap):
+            dy = dy_piece[DIRECT]
+            total = keep.tile([P, LANES, PIECE], F32, name="total", align_bytes=64)
+            grouped = keep.tile([P, PIECE * LANES], BF16, name=f"grouped{DIRECT}", align_bytes=64)
             halves = [slice(0, PIECE // 2), slice(PIECE // 2, PIECE)]
             for half in halves:
-                nc.vector.tensor_tensor(total[:, :, half], dy_piece[k][:, :, half], gap[:, :, half], ADD)
+                nc.vector.tensor_tensor(total[:, :, half], dy[:, :, half], gap[:, :, half], ADD)
             for half in halves:
                 nc.vector.tensor_tensor(
-                    grouped[:, LANES * half.start : LANES * half.stop].rearrange("p (s i j) -> p s j i", i=2, j=LANES),
-                    total[:, :, half].rearrange("p j (s i) -> p s j i", i=2),
-                    spread[k][:, :, half].rearrange("p j (s i) -> p s j i", i=2),
+                    grouped[:, LANES * half.start : LANES * half.stop].rearrange("p (t j) -> p t j", j=LANES),
+                    total[:, :, half].rearrange("p j t -> p t j"),
+                    direct_weight[:, half, :],
                     MULT,
                 )
-            quantise_g(k, grouped)
+            quantise_g(DIRECT, grouped)
 
         def deal_weights():
             nc.vector.tensor_copy(
                 w_codes[:].bitcast(I32), w_raw[:].bitcast(I32).rearrange("p (m j) -> p j m", j=LANES)
             )
-            w_scale = keep.tile([P, LANES, P], U8, name="w_scale", tag="rest2", align_bytes=64)
-            nc.vector.tensor_copy(w_scale[:], w_scale_raw[:].rearrange("p (m j) -> p j m", j=LANES))
-            return w_scale
+            dealt = keep.tile([P, LANES, P], U8, name="w_scale", tag=f"rest{PAIRED}", align_bytes=64)
+            nc.vector.tensor_copy(dealt[:], w_scale_raw[:].rearrange("p (m j) -> p j m", j=LANES))
+            return dealt
 
-        def multiply(c, w_scale, lanes):
+        def multiply(c, lanes):
             for j in lanes:
                 nc.tensor.matmul_mx(
                     banks[c * PER_CHUNK + j][:],
@@ -211,84 +225,67 @@ def tile_attend_gvq_pl_sw_x_kernel(
                     stop=True,
                 )
 
-        def store_result(c, y, lanes, copiers):
-            tokens = slice(c * CHUNK, (c + 1) * CHUNK)
+        def store_result(c, y, lanes):
             for j in lanes:
-                copiers[j](y[:, j, :], banks[c * PER_CHUNK + j][:])
-                nc.sync.dma_start(out_view[:, j, tokens], y[:, j, :])
+                nc.scalar.copy(y[:, j, :], banks[c * PER_CHUNK + j][:])
+                nc.sync.dma_start(out_view[:, j, c * CHUNK : (c + 1) * CHUNK], y[:, j, :])
 
-        def store_planes(c, y, parts):
+        def store_planes(c, y, copiers, parts_per_store):
+            width = CHUNK // len(copiers)
             y_codes = keep.tile([P, CHUNK], U32, name=f"y_codes{c}", align_bytes=64)
-            t0 = 0
-            stored = 0
-            for width, copier, store in parts:
+            for part, copier in enumerate(copiers):
+                t0, t1 = part * width, (part + 1) * width
                 y_grouped = keep.tile([P, width * LANES], BF16, name=f"y_grouped{c}_{t0}", align_bytes=64)
                 copier(
-                    y_grouped[:].rearrange("p (s i j) -> p s j i", i=2, j=LANES),
-                    y[:, :, t0 : t0 + width].rearrange("p j (s i) -> p s j i", i=2),
+                    y_grouped[:].rearrange("p (s i j) -> p s j i", i=4, j=LANES),
+                    y[:, :, t0:t1].rearrange("p j (s i) -> p s j i", i=4),
                 )
-                cols = slice(c * CHUNK + t0, c * CHUNK + t0 + width)
-                nc.vector.quantize_mx(y_codes[:, t0 : t0 + width].bitcast(E4M3), y_scales[:, cols], y_grouped[:])
-                t0 = t0 + width
-                if store:
-                    nc.sync.dma_start(
-                        words_view[:, c * CHUNK + stored : c * CHUNK + t0], y_codes[:, stored:t0].bitcast(I32)
-                    )
-                    stored = t0
+                nc.vector.quantize_mx(
+                    y_codes[:, t0:t1].bitcast(E4M3), y_scales[:, c * CHUNK + t0 : c * CHUNK + t1], y_grouped[:]
+                )
+                if (part + 1) % parts_per_store == 0:
+                    s0 = t1 - parts_per_store * width
+                    nc.sync.dma_start(words_view[:, c * CHUNK + s0 : c * CHUNK + t1], y_codes[:, s0:t1].bitcast(I32))
 
-        def gather(j, c, target):
-            codes = offsets[:, c * CHUNK // 16 : (c + 1) * CHUNK // 16]
-            nc.vector.tensor_scalar(target, book[j][:].indirect(codes), -BETA, 0.0, MULT, ADD)
-            for i in range(PER_CHUNK):
-                k = c * PER_CHUNK + i
-                if KIND[k] != "d":
-                    add_turned(k, j, target[:, i * PIECE : (i + 1) * PIECE], k >= early_pieces, k < ahead)
-
-        picked = [keep.tile([P, LANES - 1, CHUNK], F32, name=f"picked{c}") for c in range(CHUNKS)]
-        last = [keep.tile([P, CHUNK], F32, name="picked_last0")]
-        for k in range(early_pieces):
-            add_rest(k)
+        picked = [keep.tile([P, LANES - 1, CHUNK], F32, name=f"picked{c}") for c in range(2)]
+        picked_last = [keep.tile([P, CHUNK], F32, name="picked_last0")]
+        add_inputs(0)
         for j in range(LANES - 1):
-            for c in range(CHUNKS):
+            for c in range(2):
                 gather(j, c, picked[c][:, j, :])
-        for k in range(early_pieces, ahead):
-            add_rest(k)
-        gather(LANES - 1, 0, last[0][:])
+        for k in range(1, BEFORE_LAST_PLANE):
+            add_inputs(k)
+        gather(LANES - 1, 0, picked_last[0][:])
 
-        word_copiers = [on_scalar] * PIECES
-        w_scale = None
-        gaps = {}
-        y = {}
-        for step in range(PIECES + 2):
-            if ahead <= step < PIECES:
-                if KIND[step] == "d":
-                    gaps[step] = direct_gap(step)
-                else:
-                    add_rest(step)
-            if step == 3:
-                last.append(keep.tile([P, CHUNK], F32, name="picked_last1", tag="z1", align_bytes=64))
-                gather(LANES - 1, 1, last[1][:])
-            if 1 <= step <= PIECES and KIND[step - 1] != "d":
+        for step in range(PIECES + 1):
+            if BEFORE_LAST_PLANE <= step < DIRECT:
+                add_inputs(step)
+            if step == DIRECT:
+                direct_partial = direct_gap()
+            if step == PER_CHUNK - 1:
+                picked_last.append(keep.tile([P, CHUNK], F32, name="picked_last1", tag="z1", align_bytes=64))
+                gather(LANES - 1, 1, picked_last[1][:])
+            if 1 <= step <= DIRECT:
                 round_and_turn(step - 1)
-            if step - 0 in gaps:
-                direct_g(step - 0, gaps[step - 0])
-            if step >= 2 and KIND[step - 2] != "d":
-                regroup(step - 2, word_copiers[step - 2])
-            if step == 2:
+            if step == DIRECT:
+                direct_g(direct_partial)
+            if step >= 2:
+                regroup(step - 2)
+            if step == PAIRED:
                 w_scale = deal_weights()
-            if step == 5:
-                multiply(0, w_scale, range(2))
-            if step == 7:
-                y[0] = keep.tile([P, LANES, CHUNK], F32, name="y0", tag="rest4", align_bytes=64)
-                store_result(0, y[0], range(2), [on_scalar] * 4)
-        multiply(0, w_scale, range(2, LANES))
-        multiply(1, w_scale, range(LANES))
-        store_result(0, y[0], range(2, LANES), [on_scalar] * 4)
-        store_planes(0, y[0], [(256, on_vector, False), (256, on_vector, True)])
-        y[1] = keep.tile([P, LANES, CHUNK], F32, name="y1")
-        store_result(1, y[1], range(LANES), [on_scalar] * 4)
-        store_planes(1, y[1], [(128, on_vector, False), (128, on_vector, True), (128, on_scalar, False), (128, on_scalar, True)])
-        for q in range(4):
+            if step - 2 == PER_CHUNK - 1:
+                multiply(0, range(EARLY_LANES))
+            if step == DIRECT:
+                y_first = keep.tile([P, LANES, CHUNK], F32, name="y0", tag=f"rest{PER_CHUNK}", align_bytes=64)
+                store_result(0, y_first, range(EARLY_LANES))
+        multiply(0, range(EARLY_LANES, LANES))
+        multiply(1, range(LANES))
+        store_result(0, y_first, range(EARLY_LANES, LANES))
+        store_planes(0, y_first, [nc.vector.tensor_copy] * 2, 2)
+        y_second = keep.tile([P, LANES, CHUNK], F32, name="y1")
+        store_result(1, y_second, range(LANES))
+        store_planes(1, y_second, [nc.vector.tensor_copy] * 2 + [nc.scalar.copy] * 2, 2)
+        for q in range(QUADRANTS):
             engine = nc.sync if q % 2 == 0 else nc.scalar
             engine.dma_start(
                 out_2[0, 4 * q : 4 * q + 4, :].bitcast(I32), y_scales[32 * q : 32 * q + 4, :].bitcast(I32)

@@ -26,15 +26,12 @@ QUADRANTS = 4
 PIECE = 128
 PIECES = T // PIECE
 CHUNK = 512
+CHUNKS = T // CHUNK
 PER_CHUNK = CHUNK // PIECE
+HALF = CHUNK // 2
+PER_HALF = HALF // PIECE
 CODES_PER_COLUMN = 16
-
-DIRECT = PIECES - 1
-SPLIT = PIECES - 2
-PAIRED = 2
-PLANES_BEFORE_PRELOAD = 2
-BEFORE_LAST_PLANE = 3
-EARLY_LANES = 2
+WALK = 4
 
 
 def tile_attend_gvq_pl_sw_x_kernel(
@@ -44,41 +41,33 @@ def tile_attend_gvq_pl_sw_x_kernel(
     with ExitStack() as ctx:
         keep = ctx.enter_context(tc.tile_pool(name="keep", bufs=1))
         psum = ctx.enter_context(tc.psum_pool(name="psum", bufs=1))
-        banks = [psum.tile([P, CHUNK], F32, name=f"bank{k}") for k in range(PIECES)]
-
-        tw_rows = keep.tile([P, PIECE], F32, name="tw_rows")
-        nc.sync.dma_start(tw_rows[:], tw.rearrange("r (k t) -> (r k) t", t=PIECE)[0:P, :])
-        offsets = keep.tile([P, T // CODES_PER_COLUMN], U16, name="offsets")
-        nc.sync.dma_start(offsets[:], offs)
+        banks = [psum.tile([P, CHUNK], F32, name=f"bank{b}") for b in range(CHUNKS * LANES)]
+        spare_bank = banks[-1]
 
         z_view = zT.rearrange("(p j) t -> p j t", j=LANES)
         dy_view = dyT.rearrange("(p j) t -> p j t", j=LANES)
         cb_view = cb.rearrange("(p j) c -> p j c", j=LANES)
-        w_raw = keep.tile([P, D], U32, name="w_raw")
         book = [keep.tile([P, C], F32, name=f"book{j}") for j in range(LANES)]
+        offsets = keep.tile([P, T // CODES_PER_COLUMN], U16, name="offsets")
+        tw_rows = keep.tile([P, PIECE], F32, name="tw_rows")
+        w_raw = keep.tile([P, D], U32, name="w_raw")
         w_scale_raw = keep.tile([P, D], U8, name="w_scale_raw")
         nc.vector.memset(w_scale_raw[:].bitcast(I32), 0)
-        z_piece, dy_piece = {}, {}
 
-        def load_book(planes):
-            for j in planes:
-                nc.sync.dma_start(book[j][:], cb_view[:, j, :])
-
-        def load_pieces(first, count):
-            for label, view, pieces in (("z", z_view, z_piece), ("dy", dy_view, dy_piece)):
-                loaded = keep.tile([P, LANES, count * PIECE], F32, name=f"{label}{first}", align_bytes=64)
-                nc.sync.dma_start(loaded[:], view[:, :, first * PIECE : (first + count) * PIECE])
-                for i in range(count):
-                    pieces[first + i] = loaded[:, :, i * PIECE : (i + 1) * PIECE]
-
-        load_book(range(PLANES_BEFORE_PRELOAD))
-        load_pieces(0, 1)
-        load_book(range(PLANES_BEFORE_PRELOAD, LANES))
-        load_pieces(1, 1)
-        load_pieces(PAIRED, 2)
+        nc.sync.dma_start(book[0][:], cb_view[:, 0, :])
+        nc.sync.dma_start(offsets[:], offs)
+        nc.sync.dma_start(book[1][:], cb_view[:, 1, :])
+        nc.sync.dma_start(tw_rows[:], tw.rearrange("r (k t) -> (r k) t", t=PIECE)[0:P, :])
+        for j in range(2, LANES):
+            nc.sync.dma_start(book[j][:], cb_view[:, j, :])
+        z, dy = [], []
+        for c in range(CHUNKS):
+            z.append(keep.tile([P, LANES, CHUNK], F32, name=f"z{c}", align_bytes=64))
+            nc.sync.dma_start(z[c][:], z_view[:, :, c * CHUNK : (c + 1) * CHUNK])
+            dy.append([keep.tile([P, LANES, HALF], F32, name=f"dy{c}_{h}", align_bytes=64) for h in range(2)])
+            for h in range(2):
+                nc.sync.dma_start(dy[c][h][:], dy_view[:, :, c * CHUNK + h * HALF : c * CHUNK + (h + 1) * HALF])
         nc.sync.dma_start(w_raw[:].bitcast(I32), w_words[0].rearrange("p d l -> p (d l)").bitcast(I32))
-        for k in range(PER_CHUNK, PIECES):
-            load_pieces(k, 1)
 
         identity = keep.tile([P, P], F32, name="identity")
         make_identity(nc, identity[:])
@@ -88,135 +77,138 @@ def tile_attend_gvq_pl_sw_x_kernel(
             )
 
         weight = keep.tile([P, PIECES], F32, name="weight")
-        nc.tensor.transpose(banks[DIRECT][:, 0:P], tw_rows[:], identity[:])
-        nc.scalar.activation(weight[:], banks[DIRECT][:, 0:PIECES], COPY)
-        direct_weight = keep.tile([P, PIECE, LANES], F32, name="direct_weight")
-        for j in range(LANES):
-            nc.tensor.transpose(
-                banks[DIRECT][:, j * P : (j + 1) * P], weight[:, DIRECT : DIRECT + 1].to_broadcast([P, P]), identity[:]
-            )
-        nc.scalar.copy(direct_weight[:], banks[DIRECT][:].rearrange("p (j t) -> p t j", j=LANES))
+        nc.tensor.transpose(spare_bank[:, 0:P], tw_rows[:], identity[:])
+        nc.scalar.activation(weight[:], spare_bank[:, 0:PIECES], COPY)
+        spread = keep.tile([P, CHUNKS, HALF], F32, name="spread")
+        for c in range(CHUNKS):
+            for i in range(PER_HALF):
+                k = c * PER_CHUNK + PER_HALF + i
+                place = (c * PER_HALF + i) * PIECE
+                nc.tensor.transpose(
+                    spare_bank[:, place : place + PIECE], weight[:, k : k + 1].to_broadcast([P, P]), identity[:]
+                )
+        nc.scalar.copy(spread[:].rearrange("p c t -> p (c t)"), spare_bank[:])
 
-        g_codes = [keep.tile([P, CHUNK], U32, name=f"g_codes{c}", align_bytes=64) for c in range(2)]
-        g_scales = [keep.tile([P, CHUNK], U8, name=f"g_scales{c}", align_bytes=64) for c in range(2)]
+        picked = [keep.tile([P, LANES, CHUNK], F32, name=f"picked{c}") for c in range(CHUNKS)]
+        grouped = [keep.tile([P, CHUNK * LANES], BF16, name=f"grouped{c}", align_bytes=64) for c in range(CHUNKS)]
+        g_codes = [keep.tile([P, CHUNK], U32, name=f"g_codes{c}", align_bytes=64) for c in range(CHUNKS)]
+        g_scales = [keep.tile([P, CHUNK], U8, name=f"g_scales{c}", align_bytes=64) for c in range(CHUNKS)]
         w_codes = keep.tile([P, LANES, P], U32, name="w_codes", align_bytes=64)
+        y = [keep.tile([P, LANES, CHUNK], F32, name=f"y{c}") for c in range(CHUNKS)]
         y_scales = keep.tile([P, T], U8, name="y_scales", align_bytes=64)
         out_view = out_0.rearrange("(p j) t -> p j t", j=LANES)
         words_view = out_1[0].rearrange("p t l -> p (t l)").bitcast(I32)
 
-        def add_turned(k, j, source, first_term, last_term):
-            planes = 2 if k == SPLIT else LANES
-            place = j % planes
+        def add_turned(c, i, j, source, opens=False, closes=False):
             nc.tensor.matmul(
-                banks[k + j // planes][:, place * P : (place + 1) * P],
+                banks[c * LANES + i][:, j * P : (j + 1) * P],
                 source,
                 identity[:],
-                start=first_term and place == 0,
-                stop=last_term and place == planes - 1,
+                start=opens,
+                stop=closes,
                 is_transpose=True,
             )
 
-        def gather(j, c, target):
-            codes = offsets[:, c * CHUNK // CODES_PER_COLUMN : (c + 1) * CHUNK // CODES_PER_COLUMN]
-            nc.vector.tensor_scalar(target, book[j][:].indirect(codes), -BETA, 0.0, MULT, ADD)
-            for i in range(PER_CHUNK):
-                k = c * PER_CHUNK + i
-                if k != DIRECT:
-                    add_turned(k, j, target[:, i * PIECE : (i + 1) * PIECE], k > 0, k < BEFORE_LAST_PLANE)
+        def add_z(c, i):
+            scaled = keep.tile([P, LANES, PIECE], F32, name=f"scaled{c}_{i}")
+            nc.scalar.activation(scaled[:], z[c][:, :, i * PIECE : (i + 1) * PIECE], COPY, scale=BETA)
+            for j in range(LANES):
+                add_turned(c, i, j, scaled[:, j, :])
 
-        def add_inputs(k):
-            rest = keep.tile([P, LANES, PIECE], F32, name=f"rest{k}", align_bytes=64)
-            closes = k >= BEFORE_LAST_PLANE
-            if k < PER_CHUNK:
-                nc.scalar.activation(rest[:], z_piece[k], COPY, scale=BETA)
-                for j in range(LANES):
-                    add_turned(k, j, rest[:, j, :], k == 0, False)
-                for j in range(LANES):
-                    add_turned(k, j, dy_piece[k][:, j, :], False, closes)
-                return
-            group = 2 if k == SPLIT else LANES
-            for j0 in range(0, LANES, group):
-                planes = slice(j0, j0 + group)
-                nc.vector.scalar_tensor_tensor(
-                    rest[:, planes, :], z_piece[k][:, planes, :], BETA, dy_piece[k][:, planes, :], MULT, ADD
-                )
-                for j in range(j0, j0 + group):
-                    add_turned(k, j, rest[:, j, :], False, closes)
-
-        def pair_bank(k):
-            return banks[PER_CHUNK - 1] if k == SPLIT - 1 else banks[k]
-
-        def round_and_turn(k):
+        def finish_piece(c, i):
+            bank = banks[c * LANES + i]
+            k = c * PER_CHUNK + i
+            for j in range(LANES):
+                add_turned(c, i, j, dy[c][0][:, j, i * PIECE : (i + 1) * PIECE], closes=j == LANES - 1)
             rounded = keep.tile([P, 2, P, 2], BF16, name=f"rounded{k}", align_bytes=64)
+            nc.scalar.activation(
+                rounded[:], bank[:].rearrange("t (u e p) -> t u p e", u=2, e=2), COPY, scale=weight[:, k : k + 1]
+            )
             pairs = rounded[:].rearrange("t u p e -> t (u p e)").bitcast(F32)
-            scale = weight[:, k : k + 1]
-            if k != SPLIT:
-                nc.scalar.activation(
-                    rounded[:], banks[k][:].rearrange("t (u e p) -> t u p e", u=2, e=2), COPY, scale=scale
-                )
             for u in range(2):
-                if k == SPLIT:
-                    nc.scalar.activation(
-                        rounded[:, u, :, :],
-                        banks[k + u][:, 0 : 2 * P].rearrange("t (e p) -> t p e", e=2),
-                        COPY,
-                        scale=scale,
-                    )
-                nc.tensor.transpose(pair_bank(k)[:, u * P : (u + 1) * P], pairs[:, u * P : (u + 1) * P], identity[:])
-
-        def quantise_g(k, grouped):
-            c, i = divmod(k, PER_CHUNK)
-            cols = slice(i * PIECE, (i + 1) * PIECE)
-            nc.vector.quantize_mx(g_codes[c][:, cols].bitcast(E5M2), g_scales[c][:, cols], grouped[:])
-
-        def regroup(k):
-            grouped = keep.tile([P, PIECE * LANES], BF16, name=f"grouped{k}", align_bytes=64)
+                nc.tensor.transpose(bank[:, u * P : (u + 1) * P], pairs[:, u * P : (u + 1) * P], identity[:])
             nc.scalar.copy(
-                grouped[:].bitcast(F32).rearrange("p (t u) -> p t u", u=2),
-                pair_bank(k)[:, 0 : 2 * P].rearrange("p (u t) -> p t u", u=2),
+                grouped[c][:, i * PIECE * LANES : (i + 1) * PIECE * LANES].bitcast(F32).rearrange("p (t u) -> p t u", u=2),
+                bank[:, 0 : 2 * P].rearrange("p (u t) -> p t u", u=2),
             )
-            quantise_g(k, grouped)
 
-        def direct_gap():
-            cols = slice(CHUNK - PIECE, CHUNK)
-            z = z_piece[DIRECT]
-            gap = keep.tile([P, LANES, PIECE], F32, name="gap", align_bytes=64)
-            nc.vector.scalar_tensor_tensor(
-                gap[:, 0 : LANES - 1, :], z[:, 0 : LANES - 1, :], BETA, picked[1][:, :, cols], MULT, ADD
-            )
-            nc.vector.scalar_tensor_tensor(
-                gap[:, LANES - 1, :], z[:, LANES - 1, :], BETA, picked_last[1][:, cols], MULT, ADD
-            )
+        plane_pairs = [slice(0, 2), slice(2, LANES)]
+
+        def form_gap(c):
+            gap = keep.tile([P, LANES, HALF], F32, name=f"gap{c}", align_bytes=64)
+            nc.vector.scalar_tensor_tensor(gap[:], z[c][:, :, HALF:CHUNK], BETA, picked[c][:, :, HALF:CHUNK], MULT, ADD)
             return gap
 
-        def direct_g(gap):
-            dy = dy_piece[DIRECT]
-            total = keep.tile([P, LANES, PIECE], F32, name="total", align_bytes=64)
-            grouped = keep.tile([P, PIECE * LANES], BF16, name=f"grouped{DIRECT}", align_bytes=64)
-            halves = [slice(0, PIECE // 2), slice(PIECE // 2, PIECE)]
-            for half in halves:
-                nc.vector.tensor_tensor(total[:, :, half], dy[:, :, half], gap[:, :, half], ADD)
-            for half in halves:
+        def add_dy(c, gap):
+            total = keep.tile([P, LANES, HALF], F32, name=f"total{c}", align_bytes=64)
+            for planes in plane_pairs:
+                nc.vector.tensor_tensor(total[:, planes, :], dy[c][1][:, planes, :], gap[:, planes, :], ADD)
+            return total
+
+        def weigh_and_regroup(c, total):
+            planar = keep.tile([P, LANES, HALF], BF16, name=f"planar{c}", align_bytes=64)
+            for planes in plane_pairs:
                 nc.vector.tensor_tensor(
-                    grouped[:, LANES * half.start : LANES * half.stop].rearrange("p (t j) -> p t j", j=LANES),
-                    total[:, :, half].rearrange("p j t -> p t j"),
-                    direct_weight[:, half, :],
-                    MULT,
+                    planar[:, planes, :], total[:, planes, :], spread[:, c : c + 1, :].to_broadcast([P, 2, HALF]), MULT
                 )
-            quantise_g(DIRECT, grouped)
-
-        def deal_weights():
             nc.vector.tensor_copy(
-                w_codes[:].bitcast(I32), w_raw[:].bitcast(I32).rearrange("p (m j) -> p j m", j=LANES)
+                grouped[c][:, HALF * LANES : CHUNK * LANES].rearrange("p (s i j) -> p s j i", i=WALK, j=LANES),
+                planar[:].rearrange("p j (s i) -> p s j i", i=WALK),
             )
-            dealt = keep.tile([P, LANES, P], U8, name="w_scale", tag=f"rest{PAIRED}", align_bytes=64)
-            nc.vector.tensor_copy(dealt[:], w_scale_raw[:].rearrange("p (m j) -> p j m", j=LANES))
-            return dealt
 
-        def multiply(c, lanes):
-            for j in lanes:
+        def store_result(c):
+            for j in range(LANES):
+                nc.scalar.copy(y[c][:, j, :], banks[c * LANES + j][:])
+                nc.sync.dma_start(out_view[:, j, c * CHUNK : (c + 1) * CHUNK], y[c][:, j, :])
+
+        def store_planes(c, copiers):
+            width = CHUNK // len(copiers)
+            y_codes = keep.tile([P, CHUNK], U32, name=f"y_codes{c}", align_bytes=64)
+            parts = []
+            for part, copier in enumerate(copiers):
+                t0 = part * width
+                y_grouped = keep.tile([P, width * LANES], BF16, name=f"y_grouped{c}_{t0}", align_bytes=64)
+                copier(
+                    y_grouped[:].rearrange("p (s i j) -> p s j i", i=WALK, j=LANES),
+                    y[c][:, :, t0 : t0 + width].rearrange("p j (s i) -> p s j i", i=WALK),
+                )
+                parts.append((t0, y_grouped))
+            for t0, y_grouped in parts:
+                nc.vector.quantize_mx(
+                    y_codes[:, t0 : t0 + width].bitcast(E4M3),
+                    y_scales[:, c * CHUNK + t0 : c * CHUNK + t0 + width],
+                    y_grouped[:],
+                )
+            nc.sync.dma_start(words_view[:, c * CHUNK : (c + 1) * CHUNK], y_codes[:].bitcast(I32))
+
+        for j in range(LANES):
+            for c in range(CHUNKS):
+                codes = offsets[:, c * CHUNK // CODES_PER_COLUMN : (c + 1) * CHUNK // CODES_PER_COLUMN]
+                nc.vector.tensor_scalar(picked[c][:, j, :], book[j][:].indirect(codes), -BETA, 0.0, MULT, ADD)
+                for i in range(PER_HALF):
+                    add_turned(c, i, j, picked[c][:, j, i * PIECE : (i + 1) * PIECE], opens=j == 0)
+
+        for c in range(CHUNKS):
+            gap = form_gap(c)
+            for i in range(PER_HALF):
+                add_z(c, i)
+            for i in range(PER_HALF):
+                finish_piece(c, i)
+            total = add_dy(c, gap)
+            if c == CHUNKS - 1:
+                nc.vector.tensor_copy(
+                    w_codes[:].bitcast(I32), w_raw[:].bitcast(I32).rearrange("p (m j) -> p j m", j=LANES)
+                )
+            weigh_and_regroup(c, total)
+            if c == 0:
+                w_scale = keep.tile([P, LANES, P], U8, name="w_scale", tag="gap0", align_bytes=64)
+                nc.vector.tensor_copy(w_scale[:], w_scale_raw[:].rearrange("p (m j) -> p j m", j=LANES))
+            nc.vector.quantize_mx(g_codes[c][:].bitcast(E5M2), g_scales[c][:], grouped[c][:])
+
+        for c in range(CHUNKS):
+            for j in range(LANES):
                 nc.tensor.matmul_mx(
-                    banks[c * PER_CHUNK + j][:],
+                    banks[c * LANES + j][:],
                     lhsT=w_codes[:, j, :].bitcast(E4M3),
                     lhsT_scale=w_scale[:, j, :],
                     rhs=g_codes[c][:].bitcast(E5M2),
@@ -224,67 +216,10 @@ def tile_attend_gvq_pl_sw_x_kernel(
                     start=True,
                     stop=True,
                 )
-
-        def store_result(c, y, lanes):
-            for j in lanes:
-                nc.scalar.copy(y[:, j, :], banks[c * PER_CHUNK + j][:])
-                nc.sync.dma_start(out_view[:, j, c * CHUNK : (c + 1) * CHUNK], y[:, j, :])
-
-        def store_planes(c, y, copiers, parts_per_store):
-            width = CHUNK // len(copiers)
-            y_codes = keep.tile([P, CHUNK], U32, name=f"y_codes{c}", align_bytes=64)
-            for part, copier in enumerate(copiers):
-                t0, t1 = part * width, (part + 1) * width
-                y_grouped = keep.tile([P, width * LANES], BF16, name=f"y_grouped{c}_{t0}", align_bytes=64)
-                copier(
-                    y_grouped[:].rearrange("p (s i j) -> p s j i", i=4, j=LANES),
-                    y[:, :, t0:t1].rearrange("p j (s i) -> p s j i", i=4),
-                )
-                nc.vector.quantize_mx(
-                    y_codes[:, t0:t1].bitcast(E4M3), y_scales[:, c * CHUNK + t0 : c * CHUNK + t1], y_grouped[:]
-                )
-                if (part + 1) % parts_per_store == 0:
-                    s0 = t1 - parts_per_store * width
-                    nc.sync.dma_start(words_view[:, c * CHUNK + s0 : c * CHUNK + t1], y_codes[:, s0:t1].bitcast(I32))
-
-        picked = [keep.tile([P, LANES - 1, CHUNK], F32, name=f"picked{c}") for c in range(2)]
-        picked_last = [keep.tile([P, CHUNK], F32, name="picked_last0")]
-        add_inputs(0)
-        for j in range(LANES - 1):
-            for c in range(2):
-                gather(j, c, picked[c][:, j, :])
-        for k in range(1, BEFORE_LAST_PLANE):
-            add_inputs(k)
-        gather(LANES - 1, 0, picked_last[0][:])
-
-        for step in range(PIECES + 1):
-            if BEFORE_LAST_PLANE <= step < DIRECT:
-                add_inputs(step)
-            if step == DIRECT:
-                direct_partial = direct_gap()
-            if step == PER_CHUNK - 1:
-                picked_last.append(keep.tile([P, CHUNK], F32, name="picked_last1", tag="z1", align_bytes=64))
-                gather(LANES - 1, 1, picked_last[1][:])
-            if 1 <= step <= DIRECT:
-                round_and_turn(step - 1)
-            if step == DIRECT:
-                direct_g(direct_partial)
-            if step >= 2:
-                regroup(step - 2)
-            if step == PAIRED:
-                w_scale = deal_weights()
-            if step - 2 == PER_CHUNK - 1:
-                multiply(0, range(EARLY_LANES))
-            if step == DIRECT:
-                y_first = keep.tile([P, LANES, CHUNK], F32, name="y0", tag=f"rest{PER_CHUNK}", align_bytes=64)
-                store_result(0, y_first, range(EARLY_LANES))
-        multiply(0, range(EARLY_LANES, LANES))
-        multiply(1, range(LANES))
-        store_result(0, y_first, range(EARLY_LANES, LANES))
-        store_planes(0, y_first, [nc.vector.tensor_copy] * 2, 2)
-        y_second = keep.tile([P, LANES, CHUNK], F32, name="y1")
-        store_result(1, y_second, range(LANES))
-        store_planes(1, y_second, [nc.vector.tensor_copy] * 2 + [nc.scalar.copy] * 2, 2)
+        for c in range(CHUNKS):
+            store_result(c)
+        store_planes(0, [nc.vector.tensor_copy] * 2)
+        store_planes(1, [nc.vector.tensor_copy] * 2 + [nc.scalar.copy] * 2)
         for q in range(QUADRANTS):
             engine = nc.sync if q % 2 == 0 else nc.scalar
             engine.dma_start(

from contextlib import ExitStack

import concourse.mybir as mybir
from concourse.masks import make_identity

T, C, D, DV = 1024, 2048, 512, 512
BETA = 0.25
FLOPS = 2 * DV * D * T
BYTES = 4 * (2 * DV * T + DV * C + T) + DV * D + 16 * D + 2 * 128 * T // 16 + 4 * D * T + D * T + 16 * T

F32 = mybir.dt.float32
BF16 = mybir.dt.bfloat16
I32 = mybir.dt.int32
U32 = mybir.dt.uint32
U16 = mybir.dt.uint16
U8 = mybir.dt.uint8
E4M3 = mybir.dt.float8_e4m3fn_x4
E5M2 = mybir.dt.float8_e5m2_x4
COPY = mybir.ActivationFunctionType.Copy
MULT = mybir.AluOpType.mult
ADD = mybir.AluOpType.add

P = 128
LANES = 4
QUADRANTS = 4
PIECE = 128
PIECES = T // PIECE
CHUNK = 512
CHUNKS = T // CHUNK
PER_CHUNK = CHUNK // PIECE
HALF = CHUNK // 2
PER_HALF = HALF // PIECE
CODES_PER_COLUMN = 16
WALK = 4


def tile_attend_gvq_pl_sw_x_kernel(
    tc, zT, cb, dyT, tw, w_words, w_scales, offs, out_0, out_1, out_2
):
    nc = tc.nc
    with ExitStack() as ctx:
        keep = ctx.enter_context(tc.tile_pool(name="keep", bufs=1))
        psum = ctx.enter_context(tc.psum_pool(name="psum", bufs=1))
        banks = [psum.tile([P, CHUNK], F32, name=f"bank{b}") for b in range(CHUNKS * LANES)]
        spare_bank = banks[-1]

        z_view = zT.rearrange("(p j) t -> p j t", j=LANES)
        dy_view = dyT.rearrange("(p j) t -> p j t", j=LANES)
        cb_view = cb.rearrange("(p j) c -> p j c", j=LANES)
        book = [keep.tile([P, C], F32, name=f"book{j}") for j in range(LANES)]
        offsets = keep.tile([P, T // CODES_PER_COLUMN], U16, name="offsets")
        tw_rows = keep.tile([P, PIECE], F32, name="tw_rows")
        w_raw = keep.tile([P, D], U32, name="w_raw")
        w_scale_raw = keep.tile([P, D], U8, name="w_scale_raw")
        nc.vector.memset(w_scale_raw[:].bitcast(I32), 0)

        nc.sync.dma_start(book[0][:], cb_view[:, 0, :])
        nc.sync.dma_start(offsets[:], offs)
        nc.sync.dma_start(book[1][:], cb_view[:, 1, :])
        nc.sync.dma_start(tw_rows[:], tw.rearrange("r (k t) -> (r k) t", t=PIECE)[0:P, :])
        for j in range(2, LANES):
            nc.sync.dma_start(book[j][:], cb_view[:, j, :])
        z, dy = [], []
        for c in range(CHUNKS):
            z.append(keep.tile([P, LANES, CHUNK], F32, name=f"z{c}", align_bytes=64))
            nc.sync.dma_start(z[c][:], z_view[:, :, c * CHUNK : (c + 1) * CHUNK])
            dy.append([keep.tile([P, LANES, HALF], F32, name=f"dy{c}_{h}", align_bytes=64) for h in range(2)])
            for h in range(2):
                nc.sync.dma_start(dy[c][h][:], dy_view[:, :, c * CHUNK + h * HALF : c * CHUNK + (h + 1) * HALF])
        nc.sync.dma_start(w_raw[:].bitcast(I32), w_words[0].rearrange("p d l -> p (d l)").bitcast(I32))

        identity = keep.tile([P, P], F32, name="identity")
        make_identity(nc, identity[:])
        for q in range(QUADRANTS):
            nc.gpsimd.dma_start(
                w_scale_raw[32 * q : 32 * q + 4, :].bitcast(I32), w_scales[0, 4 * q : 4 * q + 4, :].bitcast(I32)
            )

        weight = keep.tile([P, PIECES], F32, name="weight")
        nc.tensor.transpose(spare_bank[:, 0:P], tw_rows[:], identity[:])
        nc.scalar.activation(weight[:], spare_bank[:, 0:PIECES], COPY)
        spread = keep.tile([P, CHUNKS, HALF], F32, name="spread")
        for c in range(CHUNKS):
            for i in range(PER_HALF):
                k = c * PER_CHUNK + PER_HALF + i
                place = (c * PER_HALF + i) * PIECE
                nc.tensor.transpose(
                    spare_bank[:, place : place + PIECE], weight[:, k : k + 1].to_broadcast([P, P]), identity[:]
                )
        nc.scalar.copy(spread[:].rearrange("p c t -> p (c t)"), spare_bank[:])

        picked = [keep.tile([P, LANES, CHUNK], F32, name=f"picked{c}") for c in range(CHUNKS)]
        grouped = [keep.tile([P, CHUNK * LANES], BF16, name=f"grouped{c}", align_bytes=64) for c in range(CHUNKS)]
        g_codes = [keep.tile([P, CHUNK], U32, name=f"g_codes{c}", align_bytes=64) for c in range(CHUNKS)]
        g_scales = [keep.tile([P, CHUNK], U8, name=f"g_scales{c}", align_bytes=64) for c in range(CHUNKS)]
        w_codes = keep.tile([P, LANES, P], U32, name="w_codes", align_bytes=64)
        y = [keep.tile([P, LANES, CHUNK], F32, name=f"y{c}") for c in range(CHUNKS)]
        y_scales = keep.tile([P, T], U8, name="y_scales", align_bytes=64)
        out_view = out_0.rearrange("(p j) t -> p j t", j=LANES)
        words_view = out_1[0].rearrange("p t l -> p (t l)").bitcast(I32)

        def add_turned(c, i, j, source, opens=False, closes=False):
            nc.tensor.matmul(
                banks[c * LANES + i][:, j * P : (j + 1) * P],
                source,
                identity[:],
                start=opens,
                stop=closes,
                is_transpose=True,
            )

        def add_z(c, i):
            scaled = keep.tile([P, LANES, PIECE], F32, name=f"scaled{c}_{i}")
            nc.scalar.activation(scaled[:], z[c][:, :, i * PIECE : (i + 1) * PIECE], COPY, scale=BETA)
            for j in range(LANES):
                add_turned(c, i, j, scaled[:, j, :])

        def finish_piece(c, i):
            bank = banks[c * LANES + i]
            k = c * PER_CHUNK + i
            for j in range(LANES):
                add_turned(c, i, j, dy[c][0][:, j, i * PIECE : (i + 1) * PIECE], closes=j == LANES - 1)
            rounded = keep.tile([P, 2, P, 2], BF16, name=f"rounded{k}", align_bytes=64)
            nc.scalar.activation(
                rounded[:], bank[:].rearrange("t (u e p) -> t u p e", u=2, e=2), COPY, scale=weight[:, k : k + 1]
            )
            pairs = rounded[:].rearrange("t u p e -> t (u p e)").bitcast(F32)
            for u in range(2):
                nc.tensor.transpose(bank[:, u * P : (u + 1) * P], pairs[:, u * P : (u + 1) * P], identity[:])
            nc.scalar.copy(
                grouped[c][:, i * PIECE * LANES : (i + 1) * PIECE * LANES].bitcast(F32).rearrange("p (t u) -> p t u", u=2),
                bank[:, 0 : 2 * P].rearrange("p (u t) -> p t u", u=2),
            )

        plane_pairs = [slice(0, 2), slice(2, LANES)]

        def form_gap(c):
            gap = keep.tile([P, LANES, HALF], F32, name=f"gap{c}", align_bytes=64)
            nc.vector.scalar_tensor_tensor(gap[:], z[c][:, :, HALF:CHUNK], BETA, picked[c][:, :, HALF:CHUNK], MULT, ADD)
            return gap

        def add_dy(c, gap):
            total = keep.tile([P, LANES, HALF], F32, name=f"total{c}", align_bytes=64)
            for planes in plane_pairs:
                nc.vector.tensor_tensor(total[:, planes, :], dy[c][1][:, planes, :], gap[:, planes, :], ADD)
            return total

        def weigh_and_regroup(c, total):
            planar = keep.tile([P, LANES, HALF], BF16, name=f"planar{c}", align_bytes=64)
            for planes in plane_pairs:
                nc.vector.tensor_tensor(
                    planar[:, planes, :], total[:, planes, :], spread[:, c : c + 1, :].to_broadcast([P, 2, HALF]), MULT
                )
            nc.vector.tensor_copy(
                grouped[c][:, HALF * LANES : CHUNK * LANES].rearrange("p (s i j) -> p s j i", i=WALK, j=LANES),
                planar[:].rearrange("p j (s i) -> p s j i", i=WALK),
            )

        def store_result(c):
            for j in range(LANES):
                nc.scalar.copy(y[c][:, j, :], banks[c * LANES + j][:])
                nc.sync.dma_start(out_view[:, j, c * CHUNK : (c + 1) * CHUNK], y[c][:, j, :])

        def store_planes(c, copiers):
            width = CHUNK // len(copiers)
            y_codes = keep.tile([P, CHUNK], U32, name=f"y_codes{c}", align_bytes=64)
            parts = []
            for part, copier in enumerate(copiers):
                t0 = part * width
                y_grouped = keep.tile([P, width * LANES], BF16, name=f"y_grouped{c}_{t0}", align_bytes=64)
                copier(
                    y_grouped[:].rearrange("p (s i j) -> p s j i", i=WALK, j=LANES),
                    y[c][:, :, t0 : t0 + width].rearrange("p j (s i) -> p s j i", i=WALK),
                )
                parts.append((t0, y_grouped))
            for t0, y_grouped in parts:
                nc.vector.quantize_mx(
                    y_codes[:, t0 : t0 + width].bitcast(E4M3),
                    y_scales[:, c * CHUNK + t0 : c * CHUNK + t0 + width],
                    y_grouped[:],
                )
            nc.sync.dma_start(words_view[:, c * CHUNK : (c + 1) * CHUNK], y_codes[:].bitcast(I32))

        for j in range(LANES):
            for c in range(CHUNKS):
                codes = offsets[:, c * CHUNK // CODES_PER_COLUMN : (c + 1) * CHUNK // CODES_PER_COLUMN]
                nc.vector.tensor_scalar(picked[c][:, j, :], book[j][:].indirect(codes), -BETA, 0.0, MULT, ADD)
                for i in range(PER_HALF):
                    add_turned(c, i, j, picked[c][:, j, i * PIECE : (i + 1) * PIECE], opens=j == 0)

        for c in range(CHUNKS):
            gap = form_gap(c)
            for i in range(PER_HALF):
                add_z(c, i)
            for i in range(PER_HALF):
                finish_piece(c, i)
            total = add_dy(c, gap)
            if c == CHUNKS - 1:
                nc.vector.tensor_copy(
                    w_codes[:].bitcast(I32), w_raw[:].bitcast(I32).rearrange("p (m j) -> p j m", j=LANES)
                )
            weigh_and_regroup(c, total)
            if c == 0:
                w_scale = keep.tile([P, LANES, P], U8, name="w_scale", tag="gap0", align_bytes=64)
                nc.vector.tensor_copy(w_scale[:], w_scale_raw[:].rearrange("p (m j) -> p j m", j=LANES))
            nc.vector.quantize_mx(g_codes[c][:].bitcast(E5M2), g_scales[c][:], grouped[c][:])

        for c in range(CHUNKS):
            for j in range(LANES):
                nc.tensor.matmul_mx(
                    banks[c * LANES + j][:],
                    lhsT=w_codes[:, j, :].bitcast(E4M3),
                    lhsT_scale=w_scale[:, j, :],
                    rhs=g_codes[c][:].bitcast(E5M2),
                    rhs_scale=g_scales[c][:],
                    start=True,
                    stop=True,
                )
        for c in range(CHUNKS):
            store_result(c)
        store_planes(0, [nc.vector.tensor_copy] * 2)
        store_planes(1, [nc.vector.tensor_copy] * 2 + [nc.scalar.copy] * 2)
        for q in range(QUADRANTS):
            engine = nc.sync if q % 2 == 0 else nc.scalar
            engine.dma_start(
                out_2[0, 4 * q : 4 * q + 4, :].bitcast(I32), y_scales[32 * q : 32 * q + 4, :].bitcast(I32)
            )
